import numpy as np
import ml_dtypes


def mxq(x, axis, fmt="e4m3"):
    dtype, down = {"e4m3": (ml_dtypes.float8_e4m3fn, 7), "e5m2": (ml_dtypes.float8_e5m2, 14)}[fmt]
    v = np.moveaxis(np.asarray(x, np.float32).astype(ml_dtypes.bfloat16).astype(np.float64), axis, -1)
    blocks = v.reshape(v.shape[:-1] + (-1, 32))
    amax = np.abs(blocks).max(-1, keepdims=True)
    byte = np.maximum(np.where(amax > 0, np.frexp(amax)[1] - 1 + 127, 0) - down, 1)
    scale = np.exp2(byte - 127.0)
    codes = (blocks / scale).astype(np.float32).astype(dtype).astype(np.float64)
    return np.moveaxis((codes * scale).reshape(v.shape), -1, axis)


WIDE = False


def mx_kscale(k):
    if not WIDE:
        return np.ones(k)
    levels = np.array([30, -30])
    if k % 512:
        return np.exp2(np.random.permutation(np.resize(levels, k // 32))).repeat(32)
    a = np.empty((k // 512, 16))
    for p in range(k // 512):
        a[p, :8] = np.random.permutation(np.resize(levels, 8))
        for g in range(8):
            far = levels[np.abs(levels - a[p, g]) >= 10]
            a[p, g + 8] = far[np.random.randint(len(far))]
    return np.exp2(a.ravel()).repeat(32)


BF16 = ml_dtypes.bfloat16


def bf(x):
    return np.asarray(x, np.float32).astype(BF16)


def f64(x):
    return np.asarray(x).astype(np.float64)


M, P, N, D = 1024, 2048, 1024, 1024


def setup_inputs():
    s = mx_kscale(P)
    t = mx_kscale(N)
    v = mx_kscale(M)
    return {
        "dy": bf(np.random.standard_normal((M, P)) * s),
        "c": bf(np.random.standard_normal((N, P)) / np.sqrt(P) / s),
        "ds_next": bf(np.random.standard_normal((M, N))),
        "decay": bf(np.random.uniform(0.5, 0.95, (N,))),
        "delta": bf(np.random.uniform(0.5, 1.5, (M, N)) * t * v[:, None]),
        "b": bf(np.random.standard_normal((D, N)) / np.sqrt(N) / t),
        "u": bf(np.random.standard_normal((M, D)) / np.sqrt(M) / v[:, None]),
    }


def reference(dy, c, ds_next, decay, delta, b, u):
    r = mxq(f64(dy), 1, "e5m2") @ mxq(f64(c), 1, "e4m3").T
    ds = r + f64(decay) * f64(ds_next)
    dz = ds * f64(delta)
    du = mxq(dz, 1, "e5m2") @ mxq(f64(b), 1, "e4m3").T
    db = mxq(f64(u), 0, "e4m3").T @ mxq(dz, 0, "e5m2")
    return du, db

@@ -1,0 +1,395 @@
+from contextlib import ExitStack
+
+import concourse.mybir as mybir
+from concourse.masks import make_identity
+
+M, P_CH, N, D = 1024, 2048, 1024, 1024
+FLOPS = 2 * M * N * P_CH + 2 * M * N * D + 2 * M * N * D
+
+F32 = mybir.dt.float32
+BF16 = mybir.dt.bfloat16
+U32 = mybir.dt.uint32
+U8 = mybir.dt.uint8
+E4 = mybir.dt.float8_e4m3fn_x4
+E5 = mybir.dt.float8_e5m2_x4
+MULT = mybir.AluOpType.mult
+ADD = mybir.AluOpType.add
+
+
+def tile_state_space_backward_s6_kernel(tc, dy, c, ds_next, decay, delta, b, u, du, db):
+    nc = tc.nc
+    with ExitStack() as ctx:
+        keep = ctx.enter_context(tc.tile_pool(name="keep", bufs=1))
+        rows = ctx.enter_context(tc.tile_pool(name="rows", bufs=13))
+        big = ctx.enter_context(tc.tile_pool(name="big", bufs=6))
+        stage = ctx.enter_context(tc.tile_pool(name="stage", bufs=5))
+        dzp = ctx.enter_context(tc.tile_pool(name="dzp", bufs=2))
+        psum = ctx.enter_context(tc.psum_pool(name="psum", bufs=4))
+        ctx.enter_context(tc.manual_schedule())
+
+        c_v = c.rearrange("(a p) k -> p a k", p=128)
+        dy_v = dy.rearrange("(g p t) k -> g p t k", g=2, t=4)
+        ds_v = ds_next.rearrange("(g p t) n -> g p t n", g=2, t=4)
+        delta_v = delta.rearrange("(g p t) n -> g p t n", g=2, t=4)
+        b_v = b.rearrange("(w a p) n -> w p a n", w=2, p=128)
+        u_v = u.rearrange("(g p j) d -> g p j d", g=2, j=4)
+        du_v = du.rearrange("(g p t) d -> g p t d", g=2, t=4)
+        db_v = db.rearrange("(a p) n -> p a n", p=128)
+
+        dec_rows = keep.tile([128, 128], BF16, name="dec_rows")
+        nc.vector.memset(dec_rows[:], 0.0)
+        ident = keep.tile([128, 128], F32, name="ident")
+        make_identity(nc, ident[:])
+        ident_h = keep.tile([128, 128], BF16, name="ident_h")
+        nc.vector.tensor_copy(out=ident_h[:], in_=ident[:])
+
+        def codes(name, width, e):
+            w = keep.tile([128, width], U32, name=name + "_codes", align_bytes=64)
+            s = keep.tile([128, width], U8, name=name + "_scales", align_bytes=64)
+            return w, s, e
+
+        c_q = [codes("c%d" % h, 4 * 512, E4) for h in range(2)]
+        dy_q = [[codes("dy%d%d" % (g, t), 512, E5) for t in range(4)] for g in range(2)]
+        b_q = [codes("b%d" % w, 2 * 512, E4) for w in range(2)]
+        u_q = [codes("u%d" % g, 1024, E4) for g in range(2)]
+        dzm_q = [[codes("dzm%d%d" % (g, h), 512, E5) for h in range(2)] for g in range(2)]
+        dzt_q = [[codes("dzt%d%d" % (g, h), 512, E5) for h in range(2)] for g in range(2)]
+
+        def nothing():
+            pass
+
+        def quant(dst, at, n, src):
+            w, s, e = dst
+            nc.vector.quantize_mx(out=w[:, at : at + n].bitcast(e), scales=s[:, at : at + n], in_=src)
+
+        def mx(out, lhs, lat, rhs, rat, first, last):
+            lw, ls, le = lhs
+            rw, rs, re = rhs
+            nc.tensor.matmul_mx(
+                out=out,
+                lhsT=lw[:, lat : lat + 128].bitcast(le),
+                lhsT_scale=ls[:, lat : lat + 128],
+                rhs=rw[:, rat : rat + 512].bitcast(re),
+                rhs_scale=rs[:, rat : rat + 512],
+                start=first,
+                stop=last,
+            )
+
+        def copy(eng, out, in_):
+            if eng == "S":
+                nc.scalar.copy(out=out, in_=in_)
+            else:
+                nc.vector.tensor_copy(out=out, in_=in_)
+
+        c_raw, dy_raw, ds_raw, delta_raw, b_raw, u_raw = {}, {}, {}, {}, {}, {}
+
+        def load_c(a, parts=1):
+            t = rows.tile([128, 2048], BF16, name="row", align_bytes=64)
+            w = 2048 // parts
+            for i in range(parts):
+                nc.sync.dma_start(out=t[:, w * i : w * i + w], in_=c_v[:, a, w * i : w * i + w])
+            c_raw[a] = t
+
+        def load_dy(g, s, parts=1):
+            t = rows.tile([128, 2048], BF16, name="row", align_bytes=64)
+            w = 2048 // parts
+            for i in range(parts):
+                nc.sync.dma_start(out=t[:, w * i : w * i + w], in_=dy_v[g][:, s, w * i : w * i + w])
+            dy_raw[g, s] = t
+
+        def load_big(store, key, view):
+            t = big.tile([128, 4, 1024], BF16, name="bigt", align_bytes=64)
+            nc.sync.dma_start(out=t[:], in_=view)
+            store[key] = t
+
+        staged = {}
+
+        def t_rows(raw):
+            words = raw[:].bitcast(F32)
+            banks = []
+            for half in range(2):
+                bank = psum.tile([128, 2, 2, 128], F32, name="tp")
+                for cc in range(2):
+                    for e in range(2):
+                        base = 256 * (2 * half + cc)
+                        nc.tensor.transpose(bank[:, cc, e, :], words[:, base + e : base + 256 : 2], ident[:])
+                banks.append(bank)
+            return banks
+
+        def e_rows(banks, engs):
+            xt = stage.tile([128, 2048], BF16, name="xt", align_bytes=64)
+            xw = xt[:].bitcast(F32).rearrange("p (k r e) -> p k r e", k=4, e=2)
+            for half in range(2):
+                copy(engs[half], xw[:, 2 * half : 2 * half + 2], banks[half][:].rearrange("p k e r -> p k r e"))
+            return xt
+
+        def item_c(a, engs):
+            def pe():
+                staged["c", a] = t_rows(c_raw[a])
+
+            def ev():
+                staged["c", a] = e_rows(staged["c", a], engs)
+
+            def post():
+                xt = staged["c", a]
+                for k in range(4):
+                    quant(c_q[a // 4], 512 * k + 128 * (a % 4), 128, xt[:, 512 * k : 512 * k + 512])
+
+            return pe, ev, post
+
+        def item_dy(g, s, engs):
+            def pe():
+                staged["d", g, s] = t_rows(dy_raw[g, s])
+
+            def ev():
+                staged["d", g, s] = e_rows(staged["d", g, s], engs)
+
+            def post():
+                quant(dy_q[g][s], 0, 512, staged["d", g, s][:])
+
+            return pe, ev, post
+
+        def item_b(i, engs):
+            w = i // 2
+
+            def pe():
+                words = b_raw[w][:].rearrange("p a n -> p (a n)").bitcast(F32)
+                banks = []
+                for r in range(2):
+                    bank = psum.tile([128, 2, 2, 128], F32, name="tp")
+                    for cc in range(2):
+                        for e in range(2):
+                            base = 512 * (2 * (i % 2) + r) + 256 * cc
+                            nc.tensor.transpose(bank[:, cc, e, :], words[:, base + e : base + 256 : 2], ident[:])
+                    banks.append(bank)
+                staged["b", i] = banks
+
+            def ev():
+                banks = staged["b", i]
+                xt = stage.tile([128, 2048], BF16, name="xt", align_bytes=64)
+                xw = xt[:].bitcast(F32).rearrange("p (k r e) -> p k r e", k=2, e=2)
+                for r in range(2):
+                    copy(engs[r], xw[:, :, 128 * r : 128 * r + 128, :], banks[r][:].rearrange("p k e r -> p k r e"))
+                staged["b", i] = xt
+
+            def post():
+                xt = staged["b", i]
+                for k in range(2):
+                    quant(b_q[w], 512 * k + 256 * (i % 2), 256, xt[:, 1024 * k : 1024 * k + 1024])
+
+            return pe, ev, post
+
+        t1, dzi = {}, {}
+
+        def make_t1(g, h, s):
+            if s == 0:
+                t1[g, h] = dzp.tile([128, 4, 512], F32, name="t1")
+            nc.vector.tensor_tensor(
+                out=t1[g, h][:, s, :],
+                in0=ds_raw[g][:, s, 512 * h : 512 * h + 512],
+                in1=dec_bc[:, 512 * h : 512 * h + 512],
+                op=MULT,
+            )
+
+        def item_m1(g, h, s):
+            def pe():
+                acc = psum.tile([128, 512], F32, name="acc")
+                for k in range(4):
+                    mx(acc[:], dy_q[g][s], 128 * k, c_q[h], 512 * k, k == 0, k == 3)
+                staged["m", g, h, s] = acc
+
+            def ev():
+                pass
+
+            def post():
+                nc.vector.tensor_tensor(
+                    out=t1[g, h][:, s, :], in0=staged["m", g, h, s][:], in1=t1[g, h][:, s, :], op=ADD
+                )
+
+            return pe, ev, post
+
+        def mult(g, h, half):
+            if half == 0:
+                dzi[g, h] = dzp.tile([128, 512, 4], BF16, name="dzi", align_bytes=64)
+            cols = slice(256 * half, 256 * half + 256)
+            gcols = slice(512 * h + 256 * half, 512 * h + 256 * half + 256)
+            nc.vector.tensor_tensor(
+                out=dzi[g, h][:, cols, :].rearrange("p (x i) t -> p x t i", i=4),
+                in0=t1[g, h][:, :, cols].rearrange("p t (x i) -> p x t i", i=4),
+                in1=delta_raw[g][:, :, gcols].rearrange("p t (x i) -> p x t i", i=4),
+                op=MULT,
+            )
+
+        def quant_dzm(g, h):
+            quant(dzm_q[g][h], 0, 512, dzi[g, h][:].rearrange("p n t -> p (n t)"))
+
+        def item_tz(g, h, engs):
+            def pe():
+                words = dzi[g, h][:].rearrange("p n t -> p (n t)").bitcast(F32)
+                banks = []
+                for e in range(2):
+                    bank = psum.tile([128, 4, 128], F32, name="tp")
+                    for q in range(4):
+                        nc.tensor.transpose(bank[:, q, :], words[:, 2 * q + e : 1024 : 8], ident[:])
+                    banks.append(bank)
+                staged["z", g, h] = banks
+
+            def ev():
+                banks = staged["z", g, h]
+                xt = stage.tile([128, 2048], BF16, name="xt", align_bytes=64)
+                xv = xt[:].rearrange("p (v e r q) -> p v e r q", v=2, e=2, q=4)
+                for v in range(2):
+                    src = banks[v][:].rearrange("p q r -> p (q r)").bitcast(BF16)
+                    copy(engs[v], xv[:, v], src.rearrange("p (q r e) -> p e r q", q=4, e=2))
+                staged["z", g, h] = xt
+
+            def post():
+                quant(dzt_q[g][h], 0, 512, staged["z", g, h][:])
+
+            return pe, ev, post
+
+        def item_mu(g, s, w, eng):
+            def pe():
+                acc = psum.tile([128, 512], F32, name="acc")
+                for h in range(2):
+                    mx(acc[:], dzt_q[g][h], 128 * s, b_q[w], 512 * h, h == 0, h == 1)
+                staged["mu"] = acc
+
+            def ev():
+                half = rows.tile([128, 512], F32, name="row", align_bytes=64)
+                copy(eng, half[:], staged["mu"][:])
+                nc.sync.dma_start(out=du_v[g][:, s, 512 * w : 512 * w + 512], in_=half[:])
+
+            return pe, ev, nothing
+
+        def item_mb(a, h, eng):
+            def pe():
+                acc = psum.tile([128, 512], F32, name="acc")
+                for g in range(2):
+                    mx(acc[:], u_q[g], 128 * a, dzm_q[g][h], 0, g == 0, g == 1)
+                staged["mb"] = acc
+
+            def ev():
+                half = rows.tile([128, 512], F32, name="row", align_bytes=64)
+                copy(eng, half[:], staged["mb"][:])
+                nc.sync.dma_start(out=db_v[:, a, 512 * h : 512 * h + 512], in_=half[:])
+
+            return pe, ev, nothing
+
+        def u_copy(g, half, eng):
+            xt = stage.tile([128, 2048], BF16, name="xt", align_bytes=64)
+            staged["u", g, half] = xt
+            src = u_raw[g][:, :, 512 * half : 512 * half + 512]
+            copy(
+                eng,
+                xt[:].rearrange("p (x i j) -> p x j i", i=4, j=4),
+                src.rearrange("p j (x i) -> p x j i", i=4),
+            )
+
+        def u_quant(g, half):
+            quant(u_q[g], 512 * half, 512, staged["u", g, half][:])
+
+        dec = {}
+
+        def spread_decay():
+            dcol_ps = psum.tile([128, 128], BF16, name="acc")
+            nc.tensor.transpose(dcol_ps[:], dec_rows[:], ident_h[:])
+            dcol = keep.tile([128, 8], BF16, name="dcol")
+            nc.vector.tensor_copy(out=dcol[:], in_=dcol_ps[:, 0:8])
+            dec["col"] = dcol
+
+        def spread_decay2():
+            dec_ps = psum.tile([128, 8, 128], BF16, name="acc")
+            for a in range(8):
+                nc.tensor.transpose(
+                    dec_ps[:, a, :], dec["col"][:, a : a + 1].to_broadcast([128, 128]), ident_h[:]
+                )
+            nc.vector.tensor_copy(out=dec_bc[:], in_=dec_ps[:].rearrange("p a r -> p (a r)"))
+
+        dec_bc = keep.tile([128, 1024], BF16, name="dec_bc")
+        load_c(0, 2)
+        nc.sync.dma_start(out=dec_rows[0:8, :], in_=decay.rearrange("(a p) -> a p", p=128))
+        for a in range(1, 4):
+            load_c(a)
+        load_dy(0, 0)
+        load_dy(0, 1)
+        load_dy(0, 2)
+        load_big(ds_raw, 0, ds_v[0])
+        load_dy(0, 3)
+        load_c(4)
+        load_big(delta_raw, 0, delta_v[0])
+        load_c(5)
+        load_c(6)
+        load_c(7)
+
+        steps = []
+
+        def step(item, *fillers):
+            steps.append((item, fillers))
+
+        step(item_c(0, "SV"))
+        step(item_c(1, "SV"))
+        step(item_c(2, "SV"))
+        step(item_c(3, "SS"), (spread_decay,))
+        step(item_dy(0, 0, "SV"), (spread_decay2,))
+        step(item_dy(0, 1, "SV"), (load_dy, 1, 0))
+        step(item_dy(0, 2, "SS"), (load_dy, 1, 1))
+        step(item_m1(0, 0, 0), (make_t1, 0, 0, 0))
+        step(item_m1(0, 0, 1), (make_t1, 0, 0, 1))
+        step(item_dy(0, 3, "SS"), (load_dy, 1, 2), (make_t1, 0, 0, 2))
+        step(item_c(4, "SS"), (load_dy, 1, 3), (make_t1, 0, 0, 3))
+        step(item_m1(0, 0, 2), (load_big, b_raw, 0, b_v[0]), (make_t1, 0, 1, 0))
+        step(item_c(5, "SS"), (load_big, ds_raw, 1, ds_v[1]))
+        step(item_c(6, "SS"), (load_big, delta_raw, 1, delta_v[1]), (make_t1, 0, 1, 1))
+        step(item_m1(0, 0, 3), (load_big, b_raw, 1, b_v[1]))
+        step(item_c(7, "SS"), (make_t1, 0, 1, 2))
+        step(item_dy(1, 0, "SS"), (mult, 0, 0, 0))
+        step(item_dy(1, 1, "SS"), (mult, 0, 0, 1))
+        step(item_m1(0, 1, 0), (make_t1, 0, 1, 3))
+        step(item_m1(0, 1, 1), (quant_dzm, 0, 0))
+        step(item_m1(0, 1, 2), (make_t1, 1, 0, 0))
+        step(item_m1(0, 1, 3), (load_big, u_raw, 0, u_v[0]))
+        step(item_dy(1, 2, "SS"), (make_t1, 1, 0, 1))
+        step(item_dy(1, 3, "SS"), (mult, 0, 1, 0))
+        step(item_m1(1, 0, 0), (mult, 0, 1, 1), (load_big, u_raw, 1, u_v[1]))
+        step(item_m1(1, 0, 1), (make_t1, 1, 0, 2))
+        step(item_b(0, "SS"), (make_t1, 1, 0, 3))
+        step(item_tz(0, 0, "SS"), (quant_dzm, 0, 1))
+        step(item_m1(1, 0, 2), (make_t1, 1, 1, 0), (u_copy, 0, 0, "S"))
+        step(item_m1(1, 0, 3), (make_t1, 1, 1, 1))
+        step(item_b(1, "SS"), (make_t1, 1, 1, 2))
+        step(item_tz(0, 1, "SS"), (mult, 1, 0, 0))
+        step(item_m1(1, 1, 0), (mult, 1, 0, 1), (u_copy, 0, 1, "S"))
+        step(item_m1(1, 1, 1), (make_t1, 1, 1, 3))
+        step(item_b(2, "SS"))
+        step(item_b(3, "SS"), (quant_dzm, 1, 0))
+        step(item_m1(1, 1, 2), (u_quant, 0, 0), (u_copy, 1, 0, "S"))
+        step(item_m1(1, 1, 3))
+        mu0 = {
+            0: [(mult, 1, 1, 0), (u_copy, 1, 1, "S")],
+            1: [(mult, 1, 1, 1)],
+            2: [(u_quant, 0, 1)],
+            3: [(quant_dzm, 1, 1)],
+            4: [(u_quant, 1, 0)],
+            5: [(u_quant, 1, 1)],
+        }
+        for j in range(8):
+            step(item_mu(0, j % 4, j // 4, "S"), *mu0.get(j, []))
+        for a in range(8):
+            step(item_mb(a, 0, "SV"[a % 2]))
+        step(item_tz(1, 0, "SV"))
+        step(item_tz(1, 1, "SV"))
+        for a in range(8):
+            step(item_mb(a, 1, "SV"[a % 2]))
+        for j in range(8):
+            step(item_mu(1, j // 2, j % 2, "SV"[j % 2]))
+
+        last_post = nothing
+        for (pe, ev, post), fillers in steps:
+            pe()
+            ev()
+            last_post()
+            for fn, *args in fillers:
+                fn(*args)
+            last_post = post
+        last_post()

@@ -20,9 +20,10 @@ def tile_state_space_backward_s6_kernel(tc, dy, c, ds_next, decay, delta, b, u, 
     nc = tc.nc
     with ExitStack() as ctx:
         keep = ctx.enter_context(tc.tile_pool(name="keep", bufs=1))
-        rows = ctx.enter_context(tc.tile_pool(name="rows", bufs=13))
+        rows = ctx.enter_context(tc.tile_pool(name="rows", bufs=12))
         big = ctx.enter_context(tc.tile_pool(name="big", bufs=6))
-        stage = ctx.enter_context(tc.tile_pool(name="stage", bufs=5))
+        stage = ctx.enter_context(tc.tile_pool(name="stage", bufs=4))
+        wove = ctx.enter_context(tc.tile_pool(name="wove", bufs=3))
         dzp = ctx.enter_context(tc.tile_pool(name="dzp", bufs=2))
         psum = ctx.enter_context(tc.psum_pool(name="psum", bufs=4))
         ctx.enter_context(tc.manual_schedule())
@@ -96,6 +97,16 @@ def tile_state_space_backward_s6_kernel(tc, dy, c, ds_next, decay, delta, b, u, 
             for i in range(parts):
                 nc.sync.dma_start(out=t[:, w * i : w * i + w], in_=dy_v[g][:, s, w * i : w * i + w])
             dy_raw[g, s] = t
+
+        def load_parts(store, key, view, parts):
+            if key not in store:
+                store[key] = big.tile([128, 4, 1024], BF16, name="bigt", align_bytes=64)
+            for s in parts:
+                nc.sync.dma_start(out=store[key][:, s, :], in_=view[:, s, :])
+
+        def load_u(g, w):
+            u_raw[g, w] = rows.tile([128, 4, 512], BF16, name="row", align_bytes=64)
+            nc.sync.dma_start(out=u_raw[g, w][:], in_=u_v[g][:, :, 512 * w : 512 * w + 512])
 
         def load_big(store, key, view):
             t = big.tile([128, 4, 1024], BF16, name="bigt", align_bytes=64)
@@ -172,12 +183,11 @@ def tile_state_space_backward_s6_kernel(tc, dy, c, ds_next, decay, delta, b, u, 
                     copy(engs[r], xw[:, :, 128 * r : 128 * r + 128, :], banks[r][:].rearrange("p k e r -> p k r e"))
                 staged["b", i] = xt
 
-            def post():
-                xt = staged["b", i]
-                for k in range(2):
-                    quant(b_q[w], 512 * k + 256 * (i % 2), 256, xt[:, 1024 * k : 1024 * k + 1024])
+            return pe, ev, nothing
 
-            return pe, ev, post
+        def quant_b(i):
+            for k in range(2):
+                quant(b_q[i // 2], 512 * k + 256 * (i % 2), 256, staged["b", i][:, 1024 * k : 1024 * k + 1024])
 
         t1, dzi = {}, {}
 
@@ -208,40 +218,46 @@ def tile_state_space_backward_s6_kernel(tc, dy, c, ds_next, decay, delta, b, u, 
 
             return pe, ev, post
 
-        def mult(g, h, half):
-            if half == 0:
-                dzi[g, h] = dzp.tile([128, 512, 4], BF16, name="dzi", align_bytes=64)
-            cols = slice(256 * half, 256 * half + 256)
-            gcols = slice(512 * h + 256 * half, 512 * h + 256 * half + 256)
+        def mult(g, h, s):
+            if s == 0:
+                dzi[g, h] = dzp.tile([128, 4, 512], BF16, name="dz", align_bytes=64)
             nc.vector.tensor_tensor(
-                out=dzi[g, h][:, cols, :].rearrange("p (x i) t -> p x t i", i=4),
-                in0=t1[g, h][:, :, cols].rearrange("p t (x i) -> p x t i", i=4),
-                in1=delta_raw[g][:, :, gcols].rearrange("p t (x i) -> p x t i", i=4),
+                out=dzi[g, h][:, s, :],
+                in0=t1[g, h][:, s, :],
+                in1=delta_raw[g][:, s, 512 * h : 512 * h + 512],
                 op=MULT,
             )
 
+        def weave_half(key, src, half, eng):
+            if half == 0:
+                staged[key] = wove.tile([128, 2048], BF16, name="wv", align_bytes=64)
+            copy(
+                eng,
+                staged[key][:, 1024 * half : 1024 * half + 1024].rearrange("p (x i t) -> p x t i", i=4, t=4),
+                src[:, :, 256 * half : 256 * half + 256].rearrange("p t (x i) -> p x t i", i=4),
+            )
+
+        def weave(g, h, half, eng):
+            weave_half(("w", g, h), dzi[g, h], half, eng)
+
         def quant_dzm(g, h):
-            quant(dzm_q[g][h], 0, 512, dzi[g, h][:].rearrange("p n t -> p (n t)"))
+            quant(dzm_q[g][h], 0, 512, staged["w", g, h][:])
 
         def item_tz(g, h, engs):
             def pe():
-                words = dzi[g, h][:].rearrange("p n t -> p (n t)").bitcast(F32)
+                words = dzi[g, h][:].rearrange("p t n -> p (t n)").bitcast(F32)
                 banks = []
-                for e in range(2):
-                    bank = psum.tile([128, 4, 128], F32, name="tp")
-                    for q in range(4):
-                        nc.tensor.transpose(bank[:, q, :], words[:, 2 * q + e : 1024 : 8], ident[:])
+                for half in range(2):
+                    bank = psum.tile([128, 2, 2, 128], F32, name="tp")
+                    for x in range(2):
+                        for e in range(2):
+                            base = 256 * (2 * half + x)
+                            nc.tensor.transpose(bank[:, x, e, :], words[:, base + e : base + 256 : 2], ident[:])
                     banks.append(bank)
                 staged["z", g, h] = banks
 
             def ev():
-                banks = staged["z", g, h]
-                xt = stage.tile([128, 2048], BF16, name="xt", align_bytes=64)
-                xv = xt[:].rearrange("p (v e r q) -> p v e r q", v=2, e=2, q=4)
-                for v in range(2):
-                    src = banks[v][:].rearrange("p q r -> p (q r)").bitcast(BF16)
-                    copy(engs[v], xv[:, v], src.rearrange("p (q r e) -> p e r q", q=4, e=2))
-                staged["z", g, h] = xt
+                staged["z", g, h] = e_rows(staged["z", g, h], engs)
 
             def post():
                 quant(dzt_q[g][h], 0, 512, staged["z", g, h][:])
@@ -256,9 +272,15 @@ def tile_state_space_backward_s6_kernel(tc, dy, c, ds_next, decay, delta, b, u, 
                 staged["mu"] = acc
 
             def ev():
-                half = rows.tile([128, 512], F32, name="row", align_bytes=64)
-                copy(eng, half[:], staged["mu"][:])
-                nc.sync.dma_start(out=du_v[g][:, s, 512 * w : 512 * w + 512], in_=half[:])
+                if w == 0:
+                    staged["du", s] = rows.tile([128, 1024], F32, name="row", align_bytes=64)
+                row = staged["du", s]
+                half = slice(512 * w, 512 * w + 512)
+                copy(eng, row[:, half], staged["mu"][:])
+                if g == 1 and s == 3:
+                    nc.sync.dma_start(out=du_v[g][:, s, half], in_=row[:, half])
+                elif w == 1:
+                    nc.sync.dma_start(out=du_v[g][:, s, :], in_=row[:])
 
             return pe, ev, nothing
 
@@ -276,15 +298,8 @@ def tile_state_space_backward_s6_kernel(tc, dy, c, ds_next, decay, delta, b, u, 
 
             return pe, ev, nothing
 
-        def u_copy(g, half, eng):
-            xt = stage.tile([128, 2048], BF16, name="xt", align_bytes=64)
-            staged["u", g, half] = xt
-            src = u_raw[g][:, :, 512 * half : 512 * half + 512]
-            copy(
-                eng,
-                xt[:].rearrange("p (x i j) -> p x j i", i=4, j=4),
-                src.rearrange("p j (x i) -> p x j i", i=4),
-            )
+        def u_copy(g, w, half, eng):
+            weave_half(("u", g, w), u_raw[g, w], half, eng)
 
         def u_quant(g, half):
             quant(u_q[g], 512 * half, 512, staged["u", g, half][:])
@@ -309,15 +324,16 @@ def tile_state_space_backward_s6_kernel(tc, dy, c, ds_next, decay, delta, b, u, 
         dec_bc = keep.tile([128, 1024], BF16, name="dec_bc")
         load_c(0, 2)
         nc.sync.dma_start(out=dec_rows[0:8, :], in_=decay.rearrange("(a p) -> a p", p=128))
-        for a in range(1, 4):
-            load_c(a)
+        load_c(1)
+        load_c(2)
+        load_c(3)
         load_dy(0, 0)
         load_dy(0, 1)
         load_dy(0, 2)
-        load_big(ds_raw, 0, ds_v[0])
+        load_parts(ds_raw, 0, ds_v[0], [0, 1, 2, 3])
         load_dy(0, 3)
         load_c(4)
-        load_big(delta_raw, 0, delta_v[0])
+        load_parts(delta_raw, 0, delta_v[0], [0, 1, 2, 3])
         load_c(5)
         load_c(6)
         load_c(7)
@@ -332,46 +348,46 @@ def tile_state_space_backward_s6_kernel(tc, dy, c, ds_next, decay, delta, b, u, 
         step(item_c(2, "SV"))
         step(item_c(3, "SS"), (spread_decay,))
         step(item_dy(0, 0, "SV"), (spread_decay2,))
-        step(item_dy(0, 1, "SV"), (load_dy, 1, 0))
-        step(item_dy(0, 2, "SS"), (load_dy, 1, 1))
+        step(item_dy(0, 1, "SV"), (load_dy, 1, 0), (load_dy, 1, 1))
+        step(item_dy(0, 2, "SS"), (load_u, 0, 0), (load_u, 1, 0))
         step(item_m1(0, 0, 0), (make_t1, 0, 0, 0))
         step(item_m1(0, 0, 1), (make_t1, 0, 0, 1))
         step(item_dy(0, 3, "SS"), (load_dy, 1, 2), (make_t1, 0, 0, 2))
         step(item_c(4, "SS"), (load_dy, 1, 3), (make_t1, 0, 0, 3))
-        step(item_m1(0, 0, 2), (load_big, b_raw, 0, b_v[0]), (make_t1, 0, 1, 0))
-        step(item_c(5, "SS"), (load_big, ds_raw, 1, ds_v[1]))
-        step(item_c(6, "SS"), (load_big, delta_raw, 1, delta_v[1]), (make_t1, 0, 1, 1))
-        step(item_m1(0, 0, 3), (load_big, b_raw, 1, b_v[1]))
-        step(item_c(7, "SS"), (make_t1, 0, 1, 2))
-        step(item_dy(1, 0, "SS"), (mult, 0, 0, 0))
-        step(item_dy(1, 1, "SS"), (mult, 0, 0, 1))
-        step(item_m1(0, 1, 0), (make_t1, 0, 1, 3))
-        step(item_m1(0, 1, 1), (quant_dzm, 0, 0))
-        step(item_m1(0, 1, 2), (make_t1, 1, 0, 0))
-        step(item_m1(0, 1, 3), (load_big, u_raw, 0, u_v[0]))
-        step(item_dy(1, 2, "SS"), (make_t1, 1, 0, 1))
-        step(item_dy(1, 3, "SS"), (mult, 0, 1, 0))
-        step(item_m1(1, 0, 0), (mult, 0, 1, 1), (load_big, u_raw, 1, u_v[1]))
-        step(item_m1(1, 0, 1), (make_t1, 1, 0, 2))
-        step(item_b(0, "SS"), (make_t1, 1, 0, 3))
-        step(item_tz(0, 0, "SS"), (quant_dzm, 0, 1))
-        step(item_m1(1, 0, 2), (make_t1, 1, 1, 0), (u_copy, 0, 0, "S"))
-        step(item_m1(1, 0, 3), (make_t1, 1, 1, 1))
-        step(item_b(1, "SS"), (make_t1, 1, 1, 2))
-        step(item_tz(0, 1, "SS"), (mult, 1, 0, 0))
-        step(item_m1(1, 1, 0), (mult, 1, 0, 1), (u_copy, 0, 1, "S"))
-        step(item_m1(1, 1, 1), (make_t1, 1, 1, 3))
-        step(item_b(2, "SS"))
-        step(item_b(3, "SS"), (quant_dzm, 1, 0))
-        step(item_m1(1, 1, 2), (u_quant, 0, 0), (u_copy, 1, 0, "S"))
-        step(item_m1(1, 1, 3))
+        step(item_m1(0, 0, 2), (make_t1, 0, 1, 0), (load_big, ds_raw, 1, ds_v[1]), (load_big, b_raw, 0, b_v[0]))
+        step(item_c(5, "SS"), (load_big, delta_raw, 1, delta_v[1]), (mult, 0, 0, 0))
+        step(item_c(6, "SS"), (load_u, 0, 1), (load_u, 1, 1), (make_t1, 0, 1, 1))
+        step(item_m1(0, 0, 3), (mult, 0, 0, 1))
+        step(item_c(7, "SS"), (load_big, b_raw, 1, b_v[1]), (mult, 0, 0, 2))
+        step(item_dy(1, 0, "SS"), (make_t1, 0, 1, 2), (mult, 0, 0, 3))
+        step(item_dy(1, 1, "SS"), (make_t1, 0, 1, 3))
+        step(item_m1(0, 1, 0), (u_copy, 0, 0, 0, "S"))
+        step(item_m1(0, 1, 1), (make_t1, 1, 0, 0), (u_copy, 0, 0, 1, "S"))
+        step(item_m1(0, 1, 2), (mult, 0, 1, 0), (weave, 0, 0, 0, "S"))
+        step(item_m1(0, 1, 3), (mult, 0, 1, 1), (weave, 0, 0, 1, "S"))
+        step(item_dy(1, 2, "SS"), (make_t1, 1, 0, 1), (mult, 0, 1, 2))
+        step(item_dy(1, 3, "SS"), (make_t1, 1, 0, 2), (mult, 0, 1, 3))
+        step(item_m1(1, 0, 0), (u_quant, 0, 0), (u_copy, 1, 0, 0, "S"))
+        step(item_m1(1, 0, 1), (make_t1, 1, 0, 3), (u_copy, 1, 0, 1, "S"))
+        step(item_b(0, "SS"), (mult, 1, 0, 0))
+        step(item_tz(0, 0, "SS"), (quant_dzm, 0, 0))
+        step(item_m1(1, 0, 2), (make_t1, 1, 1, 0), (mult, 1, 0, 1), (weave, 0, 1, 0, "S"))
+        step(item_m1(1, 0, 3), (make_t1, 1, 1, 1), (quant_b, 0), (weave, 0, 1, 1, "S"))
+        step(item_b(1, "SS"), (make_t1, 1, 1, 2), (mult, 1, 0, 2))
+        step(item_tz(0, 1, "SS"), (mult, 1, 0, 3), (u_quant, 1, 0))
+        step(item_m1(1, 1, 0), (quant_b, 1), (u_copy, 0, 1, 0, "S"))
+        step(item_m1(1, 1, 1), (make_t1, 1, 1, 3), (u_copy, 0, 1, 1, "S"))
+        step(item_b(2, "SS"), (quant_dzm, 0, 1))
+        step(item_b(3, "SS"), (mult, 1, 1, 0))
+        step(item_m1(1, 1, 2), (mult, 1, 1, 1), (weave, 1, 0, 0, "S"))
+        step(item_m1(1, 1, 3), (quant_b, 2), (weave, 1, 0, 1, "S"))
         mu0 = {
-            0: [(mult, 1, 1, 0), (u_copy, 1, 1, "S")],
-            1: [(mult, 1, 1, 1)],
-            2: [(u_quant, 0, 1)],
-            3: [(quant_dzm, 1, 1)],
-            4: [(u_quant, 1, 0)],
-            5: [(u_quant, 1, 1)],
+            0: [(mult, 1, 1, 2), (quant_b, 3)],
+            1: [(mult, 1, 1, 3), (u_quant, 0, 1)],
+            2: [(quant_dzm, 1, 0), (weave, 1, 1, 0, "V"), (weave, 1, 1, 1, "V")],
+            4: [(u_copy, 1, 1, 0, "V"), (u_copy, 1, 1, 1, "V")],
+            5: [(quant_dzm, 1, 1)],
+            6: [(u_quant, 1, 1)],
         }
         for j in range(8):
             step(item_mu(0, j % 4, j // 4, "S"), *mu0.get(j, []))

@@ -20,19 +20,20 @@ def tile_state_space_backward_s6_kernel(tc, dy, c, ds_next, decay, delta, b, u, 
     nc = tc.nc
     with ExitStack() as ctx:
         keep = ctx.enter_context(tc.tile_pool(name="keep", bufs=1))
-        rows = ctx.enter_context(tc.tile_pool(name="rows", bufs=12))
-        big = ctx.enter_context(tc.tile_pool(name="big", bufs=6))
-        stage = ctx.enter_context(tc.tile_pool(name="stage", bufs=4))
+        raw = ctx.enter_context(tc.tile_pool(name="raw", bufs=12))
+        stage = ctx.enter_context(tc.tile_pool(name="stage", bufs=3))
+        pairs = ctx.enter_context(tc.tile_pool(name="pairs", bufs=2))
         wove = ctx.enter_context(tc.tile_pool(name="wove", bufs=3))
         dzp = ctx.enter_context(tc.tile_pool(name="dzp", bufs=2))
+        codes512 = ctx.enter_context(tc.tile_pool(name="codes512", bufs=10))
         psum = ctx.enter_context(tc.psum_pool(name="psum", bufs=4))
         ctx.enter_context(tc.manual_schedule())
 
-        c_v = c.rearrange("(a p) k -> p a k", p=128)
+        c_v = c.rearrange("(h p a) k -> h p a k", h=2, a=4)
         dy_v = dy.rearrange("(g p t) k -> g p t k", g=2, t=4)
         ds_v = ds_next.rearrange("(g p t) n -> g p t n", g=2, t=4)
         delta_v = delta.rearrange("(g p t) n -> g p t n", g=2, t=4)
-        b_v = b.rearrange("(w a p) n -> w p a n", w=2, p=128)
+        b_v = b.rearrange("(w p a) n -> w p a n", w=2, a=4)
         u_v = u.rearrange("(g p j) d -> g p j d", g=2, j=4)
         du_v = du.rearrange("(g p t) d -> g p t d", g=2, t=4)
         db_v = db.rearrange("(a p) n -> p a n", p=128)
@@ -43,6 +44,8 @@ def tile_state_space_backward_s6_kernel(tc, dy, c, ds_next, decay, delta, b, u, 
         make_identity(nc, ident[:])
         ident_h = keep.tile([128, 128], BF16, name="ident_h")
         nc.vector.tensor_copy(out=ident_h[:], in_=ident[:])
+        dec_bc = keep.tile([128, 1024], BF16, name="dec_bc")
+        dcol = keep.tile([128, 8], BF16, name="dcol")
 
         def codes(name, width, e):
             w = keep.tile([128, width], U32, name=name + "_codes", align_bytes=64)
@@ -50,18 +53,19 @@ def tile_state_space_backward_s6_kernel(tc, dy, c, ds_next, decay, delta, b, u, 
             return w, s, e
 
         c_q = [codes("c%d" % h, 4 * 512, E4) for h in range(2)]
-        dy_q = [[codes("dy%d%d" % (g, t), 512, E5) for t in range(4)] for g in range(2)]
         b_q = [codes("b%d" % w, 2 * 512, E4) for w in range(2)]
         u_q = [codes("u%d" % g, 1024, E4) for g in range(2)]
-        dzm_q = [[codes("dzm%d%d" % (g, h), 512, E5) for h in range(2)] for g in range(2)]
-        dzt_q = [[codes("dzt%d%d" % (g, h), 512, E5) for h in range(2)] for g in range(2)]
-
-        def nothing():
-            pass
+        dy_q, dzm_q, dzt_q = {}, {}, {}
 
         def quant(dst, at, n, src):
             w, s, e = dst
             nc.vector.quantize_mx(out=w[:, at : at + n].bitcast(e), scales=s[:, at : at + n], in_=src)
+
+        def quant_e5m2(store, key, src):
+            w = codes512.tile([128, 512], U32, name="w512", align_bytes=64)
+            s = codes512.tile([128, 512], U8, name="s512", align_bytes=64)
+            store[key] = w, s, E5
+            quant(store[key], 0, 512, src)
 
         def mx(out, lhs, lat, rhs, rat, first, last):
             lw, ls, le = lhs
@@ -83,329 +87,514 @@ def tile_state_space_backward_s6_kernel(tc, dy, c, ds_next, decay, delta, b, u, 
                 nc.vector.tensor_copy(out=out, in_=in_)
 
         c_raw, dy_raw, ds_raw, delta_raw, b_raw, u_raw = {}, {}, {}, {}, {}, {}
+        banks, staged, accs, t1, dz, woven, out_rows = {}, {}, {}, {}, {}, {}, {}
 
-        def load_c(a, parts=1):
-            t = rows.tile([128, 2048], BF16, name="row", align_bytes=64)
-            w = 2048 // parts
-            for i in range(parts):
-                nc.sync.dma_start(out=t[:, w * i : w * i + w], in_=c_v[:, a, w * i : w * i + w])
-            c_raw[a] = t
-
-        def load_dy(g, s, parts=1):
-            t = rows.tile([128, 2048], BF16, name="row", align_bytes=64)
-            w = 2048 // parts
-            for i in range(parts):
-                nc.sync.dma_start(out=t[:, w * i : w * i + w], in_=dy_v[g][:, s, w * i : w * i + w])
-            dy_raw[g, s] = t
-
-        def load_parts(store, key, view, parts):
+        def load(store, key, view, parts):
             if key not in store:
-                store[key] = big.tile([128, 4, 1024], BF16, name="bigt", align_bytes=64)
-            for s in parts:
-                nc.sync.dma_start(out=store[key][:, s, :], in_=view[:, s, :])
+                store[key] = raw.tile([128, 4, 1024], BF16, name="raw", align_bytes=64)
+            rows = view.shape[1]
+            flat = store[key][:].rearrange("p a n -> p (a n)").rearrange("p (a n) -> p a n", a=rows)
+            for a0, a1, k0, k1 in parts:
+                nc.sync.dma_start(out=flat[:, a0:a1, k0:k1], in_=view[:, a0:a1, k0:k1])
 
-        def load_u(g, w):
-            u_raw[g, w] = rows.tile([128, 4, 512], BF16, name="row", align_bytes=64)
-            nc.sync.dma_start(out=u_raw[g, w][:], in_=u_v[g][:, :, 512 * w : 512 * w + 512])
+        def load_c(h, q, *parts):
+            load(c_raw, (h, q), c_v[h][:, 2 * q : 2 * q + 2, :], parts)
 
-        def load_big(store, key, view):
-            t = big.tile([128, 4, 1024], BF16, name="bigt", align_bytes=64)
-            nc.sync.dma_start(out=t[:], in_=view)
-            store[key] = t
+        def load_dy(g, q, *parts):
+            load(dy_raw, (g, q), dy_v[g][:, 2 * q : 2 * q + 2, :], parts)
 
-        staged = {}
+        def load_ds(g):
+            load(ds_raw, g, ds_v[g], [(0, 4, 0, 1024)])
 
-        def t_rows(raw):
-            words = raw[:].bitcast(F32)
-            banks = []
-            for half in range(2):
-                bank = psum.tile([128, 2, 2, 128], F32, name="tp")
-                for cc in range(2):
-                    for e in range(2):
-                        base = 256 * (2 * half + cc)
-                        nc.tensor.transpose(bank[:, cc, e, :], words[:, base + e : base + 256 : 2], ident[:])
-                banks.append(bank)
-            return banks
+        def load_delta(g):
+            load(delta_raw, g, delta_v[g], [(0, 4, 0, 1024)])
 
-        def e_rows(banks, engs):
-            xt = stage.tile([128, 2048], BF16, name="xt", align_bytes=64)
-            xw = xt[:].bitcast(F32).rearrange("p (k r e) -> p k r e", k=4, e=2)
-            for half in range(2):
-                copy(engs[half], xw[:, 2 * half : 2 * half + 2], banks[half][:].rearrange("p k e r -> p k r e"))
-            return xt
+        def load_b(w):
+            load(b_raw, w, b_v[w], [(0, 4, 0, 1024)])
 
-        def item_c(a, engs):
-            def pe():
-                staged["c", a] = t_rows(c_raw[a])
+        def load_u(g):
+            load(u_raw, g, u_v[g], [(0, 4, 0, 1024)])
 
-            def ev():
-                staged["c", a] = e_rows(staged["c", a], engs)
+        def load_decay():
+            nc.sync.dma_start(out=dec_rows[0:8, :], in_=decay.rearrange("(a p) -> a p", p=128))
 
-            def post():
-                xt = staged["c", a]
-                for k in range(4):
-                    quant(c_q[a // 4], 512 * k + 128 * (a % 4), 128, xt[:, 512 * k : 512 * k + 512])
+        def words_of(t):
+            return t[:].rearrange("p a n -> p (a n)").bitcast(F32)
 
-            return pe, ev, post
+        def turn(key, words, base, step):
+            bank = psum.tile([128, 2, 2, 128], F32, name="tp")
+            for x in range(2):
+                for v in range(2):
+                    lo = base + 256 * x + (v if step == 2 else 128 * v)
+                    hi = base + 256 * x + 256 if step == 2 else lo + 128
+                    nc.tensor.transpose(bank[:, x, v, :], words[:, lo:hi:step], ident[:])
+            banks[key] = bank
 
-        def item_dy(g, s, engs):
-            def pe():
-                staged["d", g, s] = t_rows(dy_raw[g, s])
+        def turn_c(h, a, half):
+            turn(("c", h, a, half), words_of(c_raw[h, a // 2]), 1024 * (a % 2) + 512 * half, 2)
 
-            def ev():
-                staged["d", g, s] = e_rows(staged["d", g, s], engs)
+        def turn_dy(g, s, half):
+            turn(("dy", g, s, half), words_of(dy_raw[g, s // 2]), 1024 * (s % 2) + 512 * half, 2)
 
-            def post():
-                quant(dy_q[g][s], 0, 512, staged["d", g, s][:])
+        def turn_b(i, half):
+            turn(("b", i, half), words_of(b_raw[i // 2]), 512 * (2 * (i % 2) + half), 2)
 
-            return pe, ev, post
+        def turn_dz(g, h, half):
+            turn(("dz", g, h, half), words_of(dz[g, h]), 512 * half, 1)
 
-        def item_b(i, engs):
-            w = i // 2
-
-            def pe():
-                words = b_raw[w][:].rearrange("p a n -> p (a n)").bitcast(F32)
-                banks = []
-                for r in range(2):
-                    bank = psum.tile([128, 2, 2, 128], F32, name="tp")
-                    for cc in range(2):
-                        for e in range(2):
-                            base = 512 * (2 * (i % 2) + r) + 256 * cc
-                            nc.tensor.transpose(bank[:, cc, e, :], words[:, base + e : base + 256 : 2], ident[:])
-                    banks.append(bank)
-                staged["b", i] = banks
-
-            def ev():
-                banks = staged["b", i]
-                xt = stage.tile([128, 2048], BF16, name="xt", align_bytes=64)
-                xw = xt[:].bitcast(F32).rearrange("p (k r e) -> p k r e", k=2, e=2)
-                for r in range(2):
-                    copy(engs[r], xw[:, :, 128 * r : 128 * r + 128, :], banks[r][:].rearrange("p k e r -> p k r e"))
-                staged["b", i] = xt
-
-            return pe, ev, nothing
-
-        def quant_b(i):
-            for k in range(2):
-                quant(b_q[i // 2], 512 * k + 256 * (i % 2), 256, staged["b", i][:, 1024 * k : 1024 * k + 1024])
-
-        t1, dzi = {}, {}
-
-        def make_t1(g, h, s):
-            if s == 0:
-                t1[g, h] = dzp.tile([128, 4, 512], F32, name="t1")
-            nc.vector.tensor_tensor(
-                out=t1[g, h][:, s, :],
-                in0=ds_raw[g][:, s, 512 * h : 512 * h + 512],
-                in1=dec_bc[:, 512 * h : 512 * h + 512],
-                op=MULT,
-            )
-
-        def item_m1(g, h, s):
-            def pe():
-                acc = psum.tile([128, 512], F32, name="acc")
-                for k in range(4):
-                    mx(acc[:], dy_q[g][s], 128 * k, c_q[h], 512 * k, k == 0, k == 3)
-                staged["m", g, h, s] = acc
-
-            def ev():
-                pass
-
-            def post():
-                nc.vector.tensor_tensor(
-                    out=t1[g, h][:, s, :], in0=staged["m", g, h, s][:], in1=t1[g, h][:, s, :], op=ADD
-                )
-
-            return pe, ev, post
-
-        def mult(g, h, s):
-            if s == 0:
-                dzi[g, h] = dzp.tile([128, 4, 512], BF16, name="dz", align_bytes=64)
-            nc.vector.tensor_tensor(
-                out=dzi[g, h][:, s, :],
-                in0=t1[g, h][:, s, :],
-                in1=delta_raw[g][:, s, 512 * h : 512 * h + 512],
-                op=MULT,
-            )
-
-        def weave_half(key, src, half, eng):
-            if half == 0:
-                staged[key] = wove.tile([128, 2048], BF16, name="wv", align_bytes=64)
+        def drain_c(h, a, half, eng):
+            if ("c", h, a // 2) not in staged:
+                staged["c", h, a // 2] = pairs.tile([128, 4096], BF16, name="xc", align_bytes=64)
+            xw = staged["c", h, a // 2][:].bitcast(F32).rearrange("p (k r v) -> p k r v", k=4, v=2)
             copy(
                 eng,
-                staged[key][:, 1024 * half : 1024 * half + 1024].rearrange("p (x i t) -> p x t i", i=4, t=4),
-                src[:, :, 256 * half : 256 * half + 256].rearrange("p t (x i) -> p x t i", i=4),
+                xw[:, 2 * half : 2 * half + 2, 128 * (a % 2) : 128 * (a % 2) + 128, :],
+                banks["c", h, a, half][:].rearrange("p k v r -> p k r v"),
             )
 
-        def weave(g, h, half, eng):
-            weave_half(("w", g, h), dzi[g, h], half, eng)
+        def drain_rows(key, half, eng):
+            if key not in staged:
+                staged[key] = stage.tile([128, 2048], BF16, name="xt", align_bytes=64)
+            xw = staged[key][:].bitcast(F32).rearrange("p (k r v) -> p k r v", k=4, v=2)
+            copy(eng, xw[:, 2 * half : 2 * half + 2], banks[key + (half,)][:].rearrange("p k v r -> p k r v"))
+
+        def drain_dy(g, s, half, eng):
+            drain_rows(("dy", g, s), half, eng)
+
+        def drain_dz(g, h, half, eng):
+            drain_rows(("dz", g, h), half, eng)
+
+        def drain_b(i, half, eng):
+            w, r0 = i // 2, 256 * (i % 2) + 128 * half
+            if ("b", w) not in staged:
+                staged["b", w] = pairs.tile([128, 4096], BF16, name="xc", align_bytes=64)
+            xw = staged["b", w][:].bitcast(F32).rearrange("p (k r v) -> p k r v", k=2, v=2)
+            copy(
+                eng,
+                xw[:, :, r0 : r0 + 128, :],
+                banks["b", i, half][:].rearrange("p k v r -> p k r v"),
+            )
+
+        def quant_c(h, j):
+            for k in range(4):
+                quant(c_q[h], 512 * k + 256 * j, 256, staged["c", h, j][:, 1024 * k : 1024 * k + 1024])
+
+        def quant_dy(g, s):
+            quant_e5m2(dy_q, (g, s), staged["dy", g, s][:])
+
+        def quant_b(w):
+            quant(b_q[w], 0, 1024, staged["b", w][:])
+
+        def quant_dzt(g, h):
+            quant_e5m2(dzt_q, (g, h), staged["dz", g, h][:])
+
+        def decay_turn():
+            accs["dcol"] = psum.tile([128, 128], BF16, name="acc")
+            nc.tensor.transpose(accs["dcol"][:], dec_rows[:], ident_h[:])
+
+        def decay_col():
+            nc.vector.tensor_copy(out=dcol[:], in_=accs["dcol"][:, 0:8])
+
+        def decay_spread():
+            accs["dec"] = psum.tile([128, 8, 128], BF16, name="acc")
+            for a in range(8):
+                nc.tensor.transpose(accs["dec"][:, a, :], dcol[:, a : a + 1].to_broadcast([128, 128]), ident_h[:])
+
+        def decay_rows():
+            nc.vector.tensor_copy(out=dec_bc[:], in_=accs["dec"][:].rearrange("p a r -> p (a r)"))
+
+        def decay_part(g, h, v):
+            if (g, h) not in t1:
+                t1[g, h] = dzp.tile([128, 4, 512], F32, name="t1")
+            nc.vector.tensor_tensor(
+                out=t1[g, h][:, :, 256 * v : 256 * v + 256].rearrange("m s (p e) -> m s p e", e=2),
+                in0=ds_raw[g][:, :, 512 * h : 512 * h + 512].rearrange("m s (p v e) -> m s v p e", v=2, e=2)[:, :, v],
+                in1=dec_bc[:, 512 * h : 512 * h + 512]
+                .rearrange("m (p v e) -> m v p e", v=2, e=2)[:, v]
+                .unsqueeze(1)
+                .to_broadcast([128, 4, 128, 2]),
+                op=MULT,
+            )
+
+        def multiply_r(g, h, s):
+            accs["r", g, h, s] = psum.tile([128, 512], F32, name="acc")
+            for k in range(4):
+                mx(accs["r", g, h, s][:], dy_q[g, s], 128 * k, c_q[h], 512 * k, k == 0, k == 3)
+
+        def add_r(g, h, s):
+            row = t1[g, h][:, s, :].rearrange("m (v p e) -> m v p e", v=2, e=2)
+            nc.vector.tensor_tensor(
+                out=row,
+                in0=accs["r", g, h, s][:].rearrange("m (v e p) -> m v p e", v=2, e=2),
+                in1=row,
+                op=ADD,
+            )
+
+        def times_delta(g, h, kind, i):
+            if (g, h) not in dz:
+                dz[g, h] = dzp.tile([128, 4, 512], BF16, name="dz", align_bytes=64)
+            to, ds = dz[g, h][:], t1[g, h][:]
+            delta_h = delta_raw[g][:, :, 512 * h : 512 * h + 512].rearrange("m s (p v e) -> m s v p e", v=2, e=2)
+            if kind == "slot":
+                to, ds = (x[:, i, :].rearrange("m (v p e) -> m v p e", v=2, e=2) for x in (to, ds))
+                factor = delta_h[:, i]
+            else:
+                half = slice(256 * i, 256 * i + 256)
+                to, ds = (x[:, :, half].rearrange("m s (p e) -> m s p e", e=2) for x in (to, ds))
+                factor = delta_h[:, :, i]
+            nc.vector.tensor_tensor(out=to, in0=ds, in1=factor, op=MULT)
+
+        def weave(key, src, n0, n1, eng):
+            if key not in woven:
+                woven[key] = wove.tile([128, 2048], BF16, name="wv", align_bytes=64)
+            copy(
+                eng,
+                woven[key][:, 4 * n0 : 4 * n1].rearrange("p (n t) -> p n t", t=4),
+                src[:, :, n0:n1].rearrange("p t n -> p n t"),
+            )
+
+        def weave_dz(g, h, n0, n1, eng):
+            weave(("dz", g, h), dz[g, h][:], n0, n1, eng)
+
+        def weave_u(g, w, n0, n1, eng):
+            weave(("u", g, w), u_raw[g][:, :, 512 * w : 512 * w + 512], n0, n1, eng)
 
         def quant_dzm(g, h):
-            quant(dzm_q[g][h], 0, 512, staged["w", g, h][:])
+            quant_e5m2(dzm_q, (g, h), woven["dz", g, h][:])
 
-        def item_tz(g, h, engs):
-            def pe():
-                words = dzi[g, h][:].rearrange("p t n -> p (t n)").bitcast(F32)
-                banks = []
-                for half in range(2):
-                    bank = psum.tile([128, 2, 2, 128], F32, name="tp")
-                    for x in range(2):
-                        for e in range(2):
-                            base = 256 * (2 * half + x)
-                            nc.tensor.transpose(bank[:, x, e, :], words[:, base + e : base + 256 : 2], ident[:])
-                    banks.append(bank)
-                staged["z", g, h] = banks
+        def quant_u(g, w):
+            quant(u_q[g], 512 * w, 512, woven["u", g, w][:])
 
-            def ev():
-                staged["z", g, h] = e_rows(staged["z", g, h], engs)
+        def multiply_du(g, s, w):
+            accs["du", g, s, w] = psum.tile([128, 512], F32, name="acc")
+            for h in range(2):
+                mx(accs["du", g, s, w][:], dzt_q[g, h], 128 * s, b_q[w], 512 * h, h == 0, h == 1)
 
-            def post():
-                quant(dzt_q[g][h], 0, 512, staged["z", g, h][:])
+        def out_tile(key):
+            if key not in out_rows:
+                out_rows[key] = raw.tile([128, 2, 512], F32, name="raw", align_bytes=64)
+            return out_rows[key]
 
-            return pe, ev, post
+        def drain_du(g, s, w, p0, p1, eng):
+            row = out_tile(("du", g, s))
+            copy(
+                eng,
+                row[:, w, :].rearrange("m (p a) -> m p a", a=4)[:, p0:p1],
+                accs["du", g, s, w][:].rearrange("m (a p) -> m p a", a=4)[:, p0:p1],
+            )
 
-        def item_mu(g, s, w, eng):
-            def pe():
-                acc = psum.tile([128, 512], F32, name="acc")
-                for h in range(2):
-                    mx(acc[:], dzt_q[g][h], 128 * s, b_q[w], 512 * h, h == 0, h == 1)
-                staged["mu"] = acc
+        def store_du(g, s):
+            nc.sync.dma_start(out=du_v[g][:, s, :], in_=out_rows["du", g, s][:].rearrange("m w d -> m (w d)"))
 
-            def ev():
-                if w == 0:
-                    staged["du", s] = rows.tile([128, 1024], F32, name="row", align_bytes=64)
-                row = staged["du", s]
-                half = slice(512 * w, 512 * w + 512)
-                copy(eng, row[:, half], staged["mu"][:])
-                if g == 1 and s == 3:
-                    nc.sync.dma_start(out=du_v[g][:, s, half], in_=row[:, half])
-                elif w == 1:
-                    nc.sync.dma_start(out=du_v[g][:, s, :], in_=row[:])
+        def store_du_half(g, s, w):
+            nc.sync.dma_start(out=du_v[g][:, s, 512 * w : 512 * w + 512], in_=out_rows["du", g, s][:, w, :])
 
-            return pe, ev, nothing
+        def multiply_db(a, h):
+            accs["db", a, h] = psum.tile([128, 512], F32, name="acc")
+            for g in range(2):
+                mx(accs["db", a, h][:], u_q[g], 128 * a, dzm_q[g, h], 0, g == 0, g == 1)
 
-        def item_mb(a, h, eng):
-            def pe():
-                acc = psum.tile([128, 512], F32, name="acc")
-                for g in range(2):
-                    mx(acc[:], u_q[g], 128 * a, dzm_q[g][h], 0, g == 0, g == 1)
-                staged["mb"] = acc
+        def drain_db(a, h, eng):
+            rows = out_tile(("db", h, a // 2))
+            copy(
+                eng,
+                rows[:, a % 2, :].rearrange("m (p v e) -> m p v e", v=2, e=2),
+                accs["db", a, h][:].rearrange("m (v p e) -> m p v e", v=2, e=2),
+            )
 
-            def ev():
-                half = rows.tile([128, 512], F32, name="row", align_bytes=64)
-                copy(eng, half[:], staged["mb"][:])
-                nc.sync.dma_start(out=db_v[:, a, 512 * h : 512 * h + 512], in_=half[:])
+        def store_db(j, h):
+            nc.sync.dma_start(out=db_v[:, 2 * j : 2 * j + 2, 512 * h : 512 * h + 512], in_=out_rows["db", h, j][:])
 
-            return pe, ev, nothing
-
-        def u_copy(g, w, half, eng):
-            weave_half(("u", g, w), u_raw[g, w], half, eng)
-
-        def u_quant(g, half):
-            quant(u_q[g], 512 * half, 512, staged["u", g, half][:])
-
-        dec = {}
-
-        def spread_decay():
-            dcol_ps = psum.tile([128, 128], BF16, name="acc")
-            nc.tensor.transpose(dcol_ps[:], dec_rows[:], ident_h[:])
-            dcol = keep.tile([128, 8], BF16, name="dcol")
-            nc.vector.tensor_copy(out=dcol[:], in_=dcol_ps[:, 0:8])
-            dec["col"] = dcol
-
-        def spread_decay2():
-            dec_ps = psum.tile([128, 8, 128], BF16, name="acc")
-            for a in range(8):
-                nc.tensor.transpose(
-                    dec_ps[:, a, :], dec["col"][:, a : a + 1].to_broadcast([128, 128]), ident_h[:]
-                )
-            nc.vector.tensor_copy(out=dec_bc[:], in_=dec_ps[:].rearrange("p a r -> p (a r)"))
-
-        dec_bc = keep.tile([128, 1024], BF16, name="dec_bc")
-        load_c(0, 2)
-        nc.sync.dma_start(out=dec_rows[0:8, :], in_=decay.rearrange("(a p) -> a p", p=128))
-        load_c(1)
-        load_c(2)
-        load_c(3)
-        load_dy(0, 0)
-        load_dy(0, 1)
-        load_dy(0, 2)
-        load_parts(ds_raw, 0, ds_v[0], [0, 1, 2, 3])
-        load_dy(0, 3)
-        load_c(4)
-        load_parts(delta_raw, 0, delta_v[0], [0, 1, 2, 3])
-        load_c(5)
-        load_c(6)
-        load_c(7)
-
-        steps = []
-
-        def step(item, *fillers):
-            steps.append((item, fillers))
-
-        step(item_c(0, "SV"))
-        step(item_c(1, "SV"))
-        step(item_c(2, "SV"))
-        step(item_c(3, "SS"), (spread_decay,))
-        step(item_dy(0, 0, "SV"), (spread_decay2,))
-        step(item_dy(0, 1, "SV"), (load_dy, 1, 0), (load_dy, 1, 1))
-        step(item_dy(0, 2, "SS"), (load_u, 0, 0), (load_u, 1, 0))
-        step(item_m1(0, 0, 0), (make_t1, 0, 0, 0))
-        step(item_m1(0, 0, 1), (make_t1, 0, 0, 1))
-        step(item_dy(0, 3, "SS"), (load_dy, 1, 2), (make_t1, 0, 0, 2))
-        step(item_c(4, "SS"), (load_dy, 1, 3), (make_t1, 0, 0, 3))
-        step(item_m1(0, 0, 2), (make_t1, 0, 1, 0), (load_big, ds_raw, 1, ds_v[1]), (load_big, b_raw, 0, b_v[0]))
-        step(item_c(5, "SS"), (load_big, delta_raw, 1, delta_v[1]), (mult, 0, 0, 0))
-        step(item_c(6, "SS"), (load_u, 0, 1), (load_u, 1, 1), (make_t1, 0, 1, 1))
-        step(item_m1(0, 0, 3), (mult, 0, 0, 1))
-        step(item_c(7, "SS"), (load_big, b_raw, 1, b_v[1]), (mult, 0, 0, 2))
-        step(item_dy(1, 0, "SS"), (make_t1, 0, 1, 2), (mult, 0, 0, 3))
-        step(item_dy(1, 1, "SS"), (make_t1, 0, 1, 3))
-        step(item_m1(0, 1, 0), (u_copy, 0, 0, 0, "S"))
-        step(item_m1(0, 1, 1), (make_t1, 1, 0, 0), (u_copy, 0, 0, 1, "S"))
-        step(item_m1(0, 1, 2), (mult, 0, 1, 0), (weave, 0, 0, 0, "S"))
-        step(item_m1(0, 1, 3), (mult, 0, 1, 1), (weave, 0, 0, 1, "S"))
-        step(item_dy(1, 2, "SS"), (make_t1, 1, 0, 1), (mult, 0, 1, 2))
-        step(item_dy(1, 3, "SS"), (make_t1, 1, 0, 2), (mult, 0, 1, 3))
-        step(item_m1(1, 0, 0), (u_quant, 0, 0), (u_copy, 1, 0, 0, "S"))
-        step(item_m1(1, 0, 1), (make_t1, 1, 0, 3), (u_copy, 1, 0, 1, "S"))
-        step(item_b(0, "SS"), (mult, 1, 0, 0))
-        step(item_tz(0, 0, "SS"), (quant_dzm, 0, 0))
-        step(item_m1(1, 0, 2), (make_t1, 1, 1, 0), (mult, 1, 0, 1), (weave, 0, 1, 0, "S"))
-        step(item_m1(1, 0, 3), (make_t1, 1, 1, 1), (quant_b, 0), (weave, 0, 1, 1, "S"))
-        step(item_b(1, "SS"), (make_t1, 1, 1, 2), (mult, 1, 0, 2))
-        step(item_tz(0, 1, "SS"), (mult, 1, 0, 3), (u_quant, 1, 0))
-        step(item_m1(1, 1, 0), (quant_b, 1), (u_copy, 0, 1, 0, "S"))
-        step(item_m1(1, 1, 1), (make_t1, 1, 1, 3), (u_copy, 0, 1, 1, "S"))
-        step(item_b(2, "SS"), (quant_dzm, 0, 1))
-        step(item_b(3, "SS"), (mult, 1, 1, 0))
-        step(item_m1(1, 1, 2), (mult, 1, 1, 1), (weave, 1, 0, 0, "S"))
-        step(item_m1(1, 1, 3), (quant_b, 2), (weave, 1, 0, 1, "S"))
-        mu0 = {
-            0: [(mult, 1, 1, 2), (quant_b, 3)],
-            1: [(mult, 1, 1, 3), (u_quant, 0, 1)],
-            2: [(quant_dzm, 1, 0), (weave, 1, 1, 0, "V"), (weave, 1, 1, 1, "V")],
-            4: [(u_copy, 1, 1, 0, "V"), (u_copy, 1, 1, 1, "V")],
-            5: [(quant_dzm, 1, 1)],
-            6: [(u_quant, 1, 1)],
-        }
-        for j in range(8):
-            step(item_mu(0, j % 4, j // 4, "S"), *mu0.get(j, []))
-        for a in range(8):
-            step(item_mb(a, 0, "SV"[a % 2]))
-        step(item_tz(1, 0, "SV"))
-        step(item_tz(1, 1, "SV"))
-        for a in range(8):
-            step(item_mb(a, 1, "SV"[a % 2]))
-        for j in range(8):
-            step(item_mu(1, j // 2, j % 2, "SV"[j % 2]))
-
-        last_post = nothing
-        for (pe, ev, post), fillers in steps:
-            pe()
-            ev()
-            last_post()
-            for fn, *args in fillers:
-                fn(*args)
-            last_post = post
-        last_post()
+        load_c(0, 1, (0, 1, 1024, 2048))
+        load_decay()
+        decay_turn()
+        decay_col()
+        turn_c(0, 2, 1)
+        decay_spread()
+        load_dy(0, 1, (1, 2, 0, 2048))
+        drain_c(0, 2, 1, "V")
+        turn_dy(0, 3, 0)
+        drain_dy(0, 3, 0, "V")
+        turn_dy(0, 3, 1)
+        drain_dy(0, 3, 1, "S")
+        decay_rows()
+        load_dy(0, 0, (1, 2, 0, 2048))
+        turn_dy(0, 1, 1)
+        turn_dy(0, 1, 0)
+        drain_dy(0, 1, 1, "V")
+        drain_dy(0, 1, 0, "V")
+        quant_dy(0, 1)
+        load_c(0, 1, (0, 1, 0, 1024))
+        turn_c(0, 2, 0)
+        drain_c(0, 2, 0, "S")
+        load_c(0, 1, (1, 2, 0, 2048))
+        quant_dy(0, 3)
+        turn_c(0, 3, 0)
+        drain_c(0, 3, 0, "V")
+        turn_c(0, 3, 1)
+        drain_c(0, 3, 1, "S")
+        quant_c(0, 1)
+        load_c(0, 0, (1, 2, 0, 2048))
+        turn_c(0, 1, 0)
+        drain_c(0, 1, 0, "S")
+        turn_c(0, 1, 1)
+        drain_c(0, 1, 1, "S")
+        load_c(0, 0, (0, 1, 0, 2048))
+        turn_c(0, 0, 0)
+        drain_c(0, 0, 0, "S")
+        load_dy(0, 1, (0, 1, 0, 2048))
+        turn_c(0, 0, 1)
+        drain_c(0, 0, 1, "S")
+        turn_dy(0, 2, 0)
+        drain_dy(0, 2, 0, "S")
+        turn_dy(0, 2, 1)
+        quant_c(0, 0)
+        multiply_r(0, 0, 1)
+        multiply_r(0, 0, 3)
+        drain_dy(0, 2, 1, "S")
+        quant_dy(0, 2)
+        load_ds(0)
+        decay_part(0, 0, 1)
+        decay_part(0, 1, 1)
+        decay_part(0, 0, 0)
+        load_c(1, 0, (0, 1, 0, 2048))
+        turn_c(1, 0, 1)
+        drain_c(1, 0, 1, "S")
+        decay_part(0, 1, 0)
+        turn_c(1, 0, 0)
+        drain_c(1, 0, 0, "S")
+        load_dy(0, 0, (0, 1, 0, 2048))
+        turn_dy(0, 0, 0)
+        turn_dy(0, 0, 1)
+        drain_dy(0, 0, 0, "S")
+        drain_dy(0, 0, 1, "S")
+        load_c(1, 1, (1, 2, 0, 2048))
+        turn_c(1, 3, 1)
+        turn_c(1, 3, 0)
+        drain_c(1, 3, 1, "S")
+        add_r(0, 0, 1)
+        drain_c(1, 3, 0, "S")
+        add_r(0, 0, 3)
+        quant_dy(0, 0)
+        load_c(1, 0, (1, 2, 0, 2048))
+        turn_c(1, 1, 0)
+        drain_c(1, 1, 0, "S")
+        turn_c(1, 1, 1)
+        drain_c(1, 1, 1, "S")
+        quant_c(1, 0)
+        load_c(1, 1, (0, 1, 0, 2048))
+        turn_c(1, 2, 1)
+        turn_c(1, 2, 0)
+        drain_c(1, 2, 1, "S")
+        drain_c(1, 2, 0, "S")
+        multiply_r(0, 0, 2)
+        multiply_r(0, 0, 0)
+        quant_c(1, 1)
+        multiply_r(0, 1, 3)
+        add_r(0, 0, 2)
+        add_r(0, 0, 0)
+        load_u(0)
+        load_delta(0)
+        weave_u(0, 1, 0, 512, "S")
+        quant_u(0, 1)
+        times_delta(0, 0, "half", 1)
+        weave_u(0, 0, 0, 512, "S")
+        add_r(0, 1, 3)
+        multiply_r(0, 1, 0)
+        add_r(0, 1, 0)
+        weave_dz(0, 0, 256, 512, "S")
+        multiply_r(0, 1, 2)
+        add_r(0, 1, 2)
+        multiply_r(0, 1, 1)
+        add_r(0, 1, 1)
+        load_dy(1, 1, (0, 2, 0, 2048))
+        turn_dy(1, 3, 1)
+        drain_dy(1, 3, 1, "S")
+        times_delta(0, 0, "half", 0)
+        turn_dy(1, 3, 0)
+        drain_dy(1, 3, 0, "S")
+        turn_dy(1, 2, 1)
+        times_delta(0, 1, "half", 1)
+        quant_dy(1, 3)
+        drain_dy(1, 2, 1, "S")
+        turn_dy(1, 2, 0)
+        drain_dy(1, 2, 0, "S")
+        quant_dy(1, 2)
+        load_dy(1, 0, (0, 2, 0, 2048))
+        turn_dy(1, 1, 1)
+        drain_dy(1, 1, 1, "S")
+        times_delta(0, 1, "half", 0)
+        turn_dy(1, 0, 0)
+        drain_dy(1, 0, 0, "S")
+        turn_dy(1, 1, 0)
+        drain_dy(1, 1, 0, "S")
+        quant_dy(1, 1)
+        quant_u(0, 0)
+        load_b(1)
+        turn_dz(0, 0, 1)
+        drain_dz(0, 0, 1, "S")
+        turn_dy(1, 0, 1)
+        drain_dy(1, 0, 1, "S")
+        turn_b(3, 0)
+        quant_dy(1, 0)
+        drain_b(3, 0, "S")
+        turn_b(2, 1)
+        drain_b(2, 1, "S")
+        turn_b(3, 1)
+        turn_b(2, 0)
+        drain_b(2, 0, "S")
+        load_ds(1)
+        decay_part(1, 0, 0)
+        decay_part(1, 1, 0)
+        weave_dz(0, 0, 0, 256, "S")
+        drain_b(3, 1, "S")
+        decay_part(1, 0, 1)
+        decay_part(1, 1, 1)
+        quant_dzm(0, 0)
+        weave_dz(0, 1, 256, 512, "S")
+        turn_dz(0, 0, 0)
+        turn_dz(0, 1, 0)
+        multiply_r(1, 0, 1)
+        add_r(1, 0, 1)
+        multiply_r(1, 0, 2)
+        add_r(1, 0, 2)
+        drain_dz(0, 0, 0, "S")
+        quant_dzt(0, 0)
+        multiply_r(1, 0, 3)
+        add_r(1, 0, 3)
+        quant_b(1)
+        drain_dz(0, 1, 0, "S")
+        load_b(0)
+        turn_b(0, 0)
+        drain_b(0, 0, "S")
+        turn_dz(0, 1, 1)
+        drain_dz(0, 1, 1, "S")
+        turn_b(1, 1)
+        turn_b(0, 1)
+        weave_dz(0, 1, 0, 256, "S")
+        turn_b(1, 0)
+        drain_b(1, 0, "S")
+        drain_b(0, 1, "S")
+        multiply_r(1, 1, 2)
+        multiply_r(1, 0, 0)
+        multiply_r(1, 1, 3)
+        add_r(1, 1, 2)
+        quant_dzt(0, 1)
+        multiply_du(0, 2, 1)
+        load_u(1)
+        load_delta(1)
+        drain_b(1, 1, "S")
+        quant_b(0)
+        multiply_du(0, 2, 0)
+        weave_u(1, 1, 0, 512, "S")
+        drain_du(0, 2, 1, 0, 128, "S")
+        drain_du(0, 2, 0, 0, 128, "S")
+        add_r(1, 0, 0)
+        multiply_du(0, 0, 1)
+        drain_du(0, 0, 1, 0, 128, "S")
+        add_r(1, 1, 3)
+        times_delta(1, 0, "half", 0)
+        quant_dzm(0, 1)
+        times_delta(1, 0, "half", 1)
+        multiply_du(0, 3, 0)
+        drain_du(0, 3, 0, 0, 128, "S")
+        quant_u(1, 1)
+        multiply_du(0, 3, 1)
+        multiply_du(0, 0, 0)
+        drain_du(0, 3, 1, 0, 128, "S")
+        multiply_du(0, 1, 0)
+        drain_du(0, 0, 0, 0, 128, "S")
+        weave_dz(1, 0, 0, 256, "V")
+        drain_du(0, 1, 0, 0, 128, "S")
+        store_du(0, 3)
+        store_du(0, 0)
+        store_du(0, 2)
+        weave_u(1, 0, 0, 512, "S")
+        multiply_r(1, 1, 0)
+        multiply_r(1, 1, 1)
+        weave_dz(1, 0, 256, 512, "V")
+        turn_dz(1, 0, 1)
+        add_r(1, 1, 0)
+        multiply_du(0, 1, 1)
+        drain_du(0, 1, 1, 0, 128, "S")
+        quant_dzm(1, 0)
+        multiply_db(4, 0)
+        drain_db(4, 0, "S")
+        add_r(1, 1, 1)
+        multiply_db(5, 0)
+        drain_db(5, 0, "S")
+        store_du(0, 1)
+        store_db(2, 0)
+        multiply_db(6, 0)
+        drain_db(6, 0, "S")
+        multiply_db(7, 0)
+        drain_db(7, 0, "S")
+        store_db(3, 0)
+        times_delta(1, 1, "slot", 2)
+        quant_u(1, 0)
+        multiply_db(1, 0)
+        drain_db(1, 0, "S")
+        multiply_db(0, 0)
+        drain_db(0, 0, "S")
+        store_db(0, 0)
+        drain_dz(1, 0, 1, "S")
+        times_delta(1, 1, "slot", 1)
+        multiply_db(2, 0)
+        drain_db(2, 0, "S")
+        multiply_db(3, 0)
+        drain_db(3, 0, "S")
+        store_db(1, 0)
+        times_delta(1, 1, "slot", 0)
+        turn_dz(1, 1, 0)
+        times_delta(1, 1, "slot", 3)
+        weave_dz(1, 1, 0, 256, "V")
+        weave_dz(1, 1, 256, 512, "V")
+        turn_dz(1, 1, 1)
+        turn_dz(1, 0, 0)
+        quant_dzm(1, 1)
+        multiply_db(4, 1)
+        drain_dz(1, 1, 0, "V")
+        drain_db(4, 1, "V")
+        drain_dz(1, 0, 0, "S")
+        multiply_db(5, 1)
+        drain_db(5, 1, "S")
+        store_db(2, 1)
+        multiply_db(1, 1)
+        drain_db(1, 1, "S")
+        multiply_db(0, 1)
+        drain_db(0, 1, "S")
+        store_db(0, 1)
+        multiply_db(2, 1)
+        drain_db(2, 1, "S")
+        multiply_db(3, 1)
+        drain_db(3, 1, "S")
+        store_db(1, 1)
+        quant_dzt(1, 0)
+        drain_dz(1, 1, 1, "V")
+        quant_dzt(1, 1)
+        multiply_du(1, 2, 0)
+        drain_du(1, 2, 0, 0, 128, "V")
+        multiply_du(1, 2, 1)
+        drain_du(1, 2, 1, 0, 128, "S")
+        multiply_db(7, 1)
+        drain_db(7, 1, "V")
+        multiply_db(6, 1)
+        store_du(1, 2)
+        multiply_du(1, 1, 0)
+        drain_db(6, 1, "V")
+        store_db(3, 1)
+        drain_du(1, 1, 0, 0, 128, "V")
+        multiply_du(1, 1, 1)
+        drain_du(1, 1, 1, 0, 128, "S")
+        store_du(1, 1)
+        multiply_du(1, 0, 0)
+        drain_du(1, 0, 0, 0, 128, "V")
+        multiply_du(1, 3, 1)
+        drain_du(1, 3, 1, 0, 128, "S")
+        store_du_half(1, 3, 1)
+        multiply_du(1, 3, 0)
+        drain_du(1, 3, 0, 0, 128, "V")
+        store_du_half(1, 3, 0)
+        multiply_du(1, 0, 1)
+        drain_du(1, 0, 1, 0, 128, "S")
+        store_du(1, 0)

@@ -33,7 +33,7 @@ def tile_state_space_backward_s6_kernel(tc, dy, c, ds_next, decay, delta, b, u, 
         dy_v = dy.rearrange("(g p t) k -> g p t k", g=2, t=4)
         ds_v = ds_next.rearrange("(g p t) n -> g p t n", g=2, t=4)
         delta_v = delta.rearrange("(g p t) n -> g p t n", g=2, t=4)
-        b_v = b.rearrange("(w p a) n -> w p a n", w=2, a=4)
+        b_v = b.rearrange("(w x p y) n -> w p x y n", w=2, x=2, y=2)
         u_v = u.rearrange("(g p j) d -> g p j d", g=2, j=4)
         du_v = du.rearrange("(g p t) d -> g p t d", g=2, t=4)
         db_v = db.rearrange("(a p) n -> p a n", p=128)
@@ -110,7 +110,8 @@ def tile_state_space_backward_s6_kernel(tc, dy, c, ds_next, decay, delta, b, u, 
             load(delta_raw, g, delta_v[g], [(0, 4, 0, 1024)])
 
         def load_b(w):
-            load(b_raw, w, b_v[w], [(0, 4, 0, 1024)])
+            b_raw[w] = raw.tile([128, 4, 1024], BF16, name="raw", align_bytes=64)
+            nc.sync.dma_start(out=b_raw[w][:].rearrange("p (x y) n -> p x y n", x=2), in_=b_v[w])
 
         def load_u(g):
             load(u_raw, g, u_v[g], [(0, 4, 0, 1024)])
@@ -275,12 +276,12 @@ def tile_state_space_backward_s6_kernel(tc, dy, c, ds_next, decay, delta, b, u, 
                 out_rows[key] = raw.tile([128, 2, 512], F32, name="raw", align_bytes=64)
             return out_rows[key]
 
-        def drain_du(g, s, w, p0, p1, eng):
+        def drain_du(g, s, w, eng):
             row = out_tile(("du", g, s))
             copy(
                 eng,
-                row[:, w, :].rearrange("m (p a) -> m p a", a=4)[:, p0:p1],
-                accs["du", g, s, w][:].rearrange("m (a p) -> m p a", a=4)[:, p0:p1],
+                row[:, w, :].rearrange("m (x p y) -> m x p y", x=2, y=2),
+                accs["du", g, s, w][:].rearrange("m (x y p) -> m x p y", x=2, y=2),
             )
 
         def store_du(g, s):
@@ -305,296 +306,296 @@ def tile_state_space_backward_s6_kernel(tc, dy, c, ds_next, decay, delta, b, u, 
         def store_db(j, h):
             nc.sync.dma_start(out=db_v[:, 2 * j : 2 * j + 2, 512 * h : 512 * h + 512], in_=out_rows["db", h, j][:])
 
-        load_c(0, 1, (0, 1, 1024, 2048))
-        load_decay()
-        decay_turn()
-        decay_col()
-        turn_c(0, 2, 1)
-        decay_spread()
-        load_dy(0, 1, (1, 2, 0, 2048))
-        drain_c(0, 2, 1, "V")
-        turn_dy(0, 3, 0)
-        drain_dy(0, 3, 0, "V")
-        turn_dy(0, 3, 1)
-        drain_dy(0, 3, 1, "S")
-        decay_rows()
         load_dy(0, 0, (1, 2, 0, 2048))
         turn_dy(0, 1, 1)
         turn_dy(0, 1, 0)
+        drain_dy(0, 1, 0, "S")
+        load_c(0, 0, (0, 1, 0, 2048))
         drain_dy(0, 1, 1, "V")
-        drain_dy(0, 1, 0, "V")
-        quant_dy(0, 1)
-        load_c(0, 1, (0, 1, 0, 1024))
-        turn_c(0, 2, 0)
-        drain_c(0, 2, 0, "S")
-        load_c(0, 1, (1, 2, 0, 2048))
+        turn_c(0, 0, 0)
+        turn_c(0, 0, 1)
+        drain_c(0, 0, 1, "S")
+        drain_c(0, 0, 0, "V")
+        load_dy(0, 1, (1, 2, 0, 2048))
+        turn_dy(0, 3, 1)
+        drain_dy(0, 3, 1, "S")
+        turn_dy(0, 3, 0)
+        drain_dy(0, 3, 0, "S")
         quant_dy(0, 3)
+        load_c(0, 1, (1, 2, 0, 2048))
         turn_c(0, 3, 0)
+        load_dy(0, 1, (0, 1, 0, 2048))
+        quant_dy(0, 1)
         drain_c(0, 3, 0, "V")
+        turn_dy(0, 2, 1)
+        drain_dy(0, 2, 1, "V")
+        load_decay()
+        decay_turn()
         turn_c(0, 3, 1)
         drain_c(0, 3, 1, "S")
-        quant_c(0, 1)
+        decay_col()
+        turn_dy(0, 2, 0)
+        drain_dy(0, 2, 0, "S")
         load_c(0, 0, (1, 2, 0, 2048))
         turn_c(0, 1, 0)
+        quant_dy(0, 2)
         drain_c(0, 1, 0, "S")
         turn_c(0, 1, 1)
         drain_c(0, 1, 1, "S")
-        load_c(0, 0, (0, 1, 0, 2048))
-        turn_c(0, 0, 0)
-        drain_c(0, 0, 0, "S")
-        load_dy(0, 1, (0, 1, 0, 2048))
-        turn_c(0, 0, 1)
-        drain_c(0, 0, 1, "S")
-        turn_dy(0, 2, 0)
-        drain_dy(0, 2, 0, "S")
-        turn_dy(0, 2, 1)
         quant_c(0, 0)
-        multiply_r(0, 0, 1)
-        multiply_r(0, 0, 3)
-        drain_dy(0, 2, 1, "S")
-        quant_dy(0, 2)
-        load_ds(0)
-        decay_part(0, 0, 1)
-        decay_part(0, 1, 1)
-        decay_part(0, 0, 0)
-        load_c(1, 0, (0, 1, 0, 2048))
-        turn_c(1, 0, 1)
-        drain_c(1, 0, 1, "S")
-        decay_part(0, 1, 0)
-        turn_c(1, 0, 0)
-        drain_c(1, 0, 0, "S")
+        load_c(0, 1, (0, 1, 1024, 2048))
+        load_c(0, 1, (0, 1, 0, 1024))
+        turn_c(0, 2, 1)
+        turn_c(0, 2, 0)
+        drain_c(0, 2, 0, "S")
+        drain_c(0, 2, 1, "S")
+        load_c(1, 1, (1, 2, 0, 2048))
+        turn_c(1, 3, 0)
+        quant_c(0, 1)
+        turn_c(1, 3, 1)
+        drain_c(1, 3, 1, "S")
+        decay_spread()
         load_dy(0, 0, (0, 1, 0, 2048))
         turn_dy(0, 0, 0)
-        turn_dy(0, 0, 1)
+        decay_rows()
         drain_dy(0, 0, 0, "S")
-        drain_dy(0, 0, 1, "S")
-        load_c(1, 1, (1, 2, 0, 2048))
-        turn_c(1, 3, 1)
-        turn_c(1, 3, 0)
-        drain_c(1, 3, 1, "S")
-        add_r(0, 0, 1)
         drain_c(1, 3, 0, "S")
-        add_r(0, 0, 3)
-        quant_dy(0, 0)
+        multiply_r(0, 0, 3)
+        turn_dy(0, 0, 1)
+        load_ds(0)
+        decay_part(0, 0, 0)
         load_c(1, 0, (1, 2, 0, 2048))
         turn_c(1, 1, 0)
         drain_c(1, 1, 0, "S")
         turn_c(1, 1, 1)
+        drain_dy(0, 0, 1, "S")
+        decay_part(0, 1, 1)
         drain_c(1, 1, 1, "S")
-        quant_c(1, 0)
+        multiply_r(0, 0, 1)
         load_c(1, 1, (0, 1, 0, 2048))
-        turn_c(1, 2, 1)
         turn_c(1, 2, 0)
-        drain_c(1, 2, 1, "S")
         drain_c(1, 2, 0, "S")
+        turn_c(1, 2, 1)
+        drain_c(1, 2, 1, "S")
+        decay_part(0, 0, 1)
+        decay_part(0, 1, 0)
+        load_c(1, 0, (0, 1, 0, 2048))
+        turn_c(1, 0, 1)
+        drain_c(1, 0, 1, "S")
+        quant_dy(0, 0)
+        turn_c(1, 0, 0)
+        add_r(0, 0, 3)
+        add_r(0, 0, 1)
+        quant_c(1, 1)
+        drain_c(1, 0, 0, "S")
+        quant_c(1, 0)
         multiply_r(0, 0, 2)
         multiply_r(0, 0, 0)
-        quant_c(1, 1)
-        multiply_r(0, 1, 3)
-        add_r(0, 0, 2)
         add_r(0, 0, 0)
+        add_r(0, 0, 2)
         load_u(0)
-        load_delta(0)
         weave_u(0, 1, 0, 512, "S")
         quant_u(0, 1)
+        load_dy(1, 0, (0, 2, 0, 2048))
+        turn_dy(1, 0, 1)
+        turn_dy(1, 0, 0)
+        drain_dy(1, 0, 0, "S")
+        turn_dy(1, 1, 1)
+        multiply_r(0, 1, 0)
+        multiply_r(0, 1, 2)
+        multiply_r(0, 1, 1)
+        load_delta(0)
+        times_delta(0, 0, "half", 0)
+        add_r(0, 1, 0)
         times_delta(0, 0, "half", 1)
         weave_u(0, 0, 0, 512, "S")
-        add_r(0, 1, 3)
-        multiply_r(0, 1, 0)
-        add_r(0, 1, 0)
-        weave_dz(0, 0, 256, 512, "S")
-        multiply_r(0, 1, 2)
-        add_r(0, 1, 2)
-        multiply_r(0, 1, 1)
+        quant_u(0, 0)
+        turn_dy(1, 1, 0)
+        turn_dz(0, 0, 1)
         add_r(0, 1, 1)
+        drain_dy(1, 0, 1, "S")
+        quant_dy(1, 0)
         load_dy(1, 1, (0, 2, 0, 2048))
-        turn_dy(1, 3, 1)
-        drain_dy(1, 3, 1, "S")
-        times_delta(0, 0, "half", 0)
-        turn_dy(1, 3, 0)
-        drain_dy(1, 3, 0, "S")
         turn_dy(1, 2, 1)
-        times_delta(0, 1, "half", 1)
-        quant_dy(1, 3)
+        weave_dz(0, 0, 0, 256, "S")
+        multiply_r(0, 1, 3)
+        drain_dy(1, 1, 1, "S")
+        drain_dy(1, 1, 0, "S")
+        add_r(0, 1, 2)
+        load_ds(1)
+        decay_part(1, 0, 1)
+        add_r(0, 1, 3)
+        quant_dy(1, 1)
+        times_delta(0, 1, "half", 0)
+        decay_part(1, 0, 0)
+        drain_dz(0, 0, 1, "S")
         drain_dy(1, 2, 1, "S")
+        weave_dz(0, 0, 256, 512, "S")
+        turn_dy(1, 3, 1)
+        turn_dz(0, 0, 0)
+        drain_dy(1, 3, 1, "S")
+        drain_dz(0, 0, 0, "S")
+        multiply_r(1, 1, 0)
+        times_delta(0, 1, "half", 1)
+        quant_dzt(0, 0)
         turn_dy(1, 2, 0)
         drain_dy(1, 2, 0, "S")
         quant_dy(1, 2)
-        load_dy(1, 0, (0, 2, 0, 2048))
-        turn_dy(1, 1, 1)
-        drain_dy(1, 1, 1, "S")
-        times_delta(0, 1, "half", 0)
-        turn_dy(1, 0, 0)
-        drain_dy(1, 0, 0, "S")
-        turn_dy(1, 1, 0)
-        drain_dy(1, 1, 0, "S")
-        quant_dy(1, 1)
-        quant_u(0, 0)
-        load_b(1)
-        turn_dz(0, 0, 1)
-        drain_dz(0, 0, 1, "S")
-        turn_dy(1, 0, 1)
-        drain_dy(1, 0, 1, "S")
-        turn_b(3, 0)
-        quant_dy(1, 0)
-        drain_b(3, 0, "S")
-        turn_b(2, 1)
-        drain_b(2, 1, "S")
-        turn_b(3, 1)
-        turn_b(2, 0)
-        drain_b(2, 0, "S")
-        load_ds(1)
-        decay_part(1, 0, 0)
-        decay_part(1, 1, 0)
-        weave_dz(0, 0, 0, 256, "S")
-        drain_b(3, 1, "S")
-        decay_part(1, 0, 1)
-        decay_part(1, 1, 1)
-        quant_dzm(0, 0)
-        weave_dz(0, 1, 256, 512, "S")
-        turn_dz(0, 0, 0)
-        turn_dz(0, 1, 0)
-        multiply_r(1, 0, 1)
-        add_r(1, 0, 1)
-        multiply_r(1, 0, 2)
-        add_r(1, 0, 2)
-        drain_dz(0, 0, 0, "S")
-        quant_dzt(0, 0)
-        multiply_r(1, 0, 3)
-        add_r(1, 0, 3)
-        quant_b(1)
-        drain_dz(0, 1, 0, "S")
         load_b(0)
-        turn_b(0, 0)
-        drain_b(0, 0, "S")
-        turn_dz(0, 1, 1)
-        drain_dz(0, 1, 1, "S")
-        turn_b(1, 1)
-        turn_b(0, 1)
-        weave_dz(0, 1, 0, 256, "S")
         turn_b(1, 0)
         drain_b(1, 0, "S")
-        drain_b(0, 1, "S")
-        multiply_r(1, 1, 2)
-        multiply_r(1, 0, 0)
-        multiply_r(1, 1, 3)
-        add_r(1, 1, 2)
-        quant_dzt(0, 1)
-        multiply_du(0, 2, 1)
+        load_b(1)
+        turn_b(2, 0)
+        drain_b(2, 0, "S")
+        turn_dy(1, 3, 0)
+        decay_part(1, 1, 1)
+        drain_dy(1, 3, 0, "S")
         load_u(1)
-        load_delta(1)
-        drain_b(1, 1, "S")
-        quant_b(0)
-        multiply_du(0, 2, 0)
         weave_u(1, 1, 0, 512, "S")
-        drain_du(0, 2, 1, 0, 128, "S")
-        drain_du(0, 2, 0, 0, 128, "S")
+        multiply_r(1, 0, 0)
         add_r(1, 0, 0)
-        multiply_du(0, 0, 1)
-        drain_du(0, 0, 1, 0, 128, "S")
-        add_r(1, 1, 3)
-        times_delta(1, 0, "half", 0)
-        quant_dzm(0, 1)
-        times_delta(1, 0, "half", 1)
-        multiply_du(0, 3, 0)
-        drain_du(0, 3, 0, 0, 128, "S")
-        quant_u(1, 1)
-        multiply_du(0, 3, 1)
-        multiply_du(0, 0, 0)
-        drain_du(0, 3, 1, 0, 128, "S")
-        multiply_du(0, 1, 0)
-        drain_du(0, 0, 0, 0, 128, "S")
-        weave_dz(1, 0, 0, 256, "V")
-        drain_du(0, 1, 0, 0, 128, "S")
-        store_du(0, 3)
-        store_du(0, 0)
-        store_du(0, 2)
-        weave_u(1, 0, 0, 512, "S")
-        multiply_r(1, 1, 0)
-        multiply_r(1, 1, 1)
-        weave_dz(1, 0, 256, 512, "V")
-        turn_dz(1, 0, 1)
+        turn_b(0, 0)
+        drain_b(0, 0, "S")
+        quant_dy(1, 3)
+        turn_dz(0, 1, 1)
+        drain_dz(0, 1, 1, "S")
+        decay_part(1, 1, 0)
+        quant_dzm(0, 0)
         add_r(1, 1, 0)
+        turn_b(3, 1)
+        multiply_r(1, 0, 2)
+        turn_b(3, 0)
+        add_r(1, 0, 2)
+        turn_b(2, 1)
+        drain_b(3, 1, "S")
+        drain_b(3, 0, "S")
+        drain_b(2, 1, "S")
+        quant_b(1)
+        turn_dz(0, 1, 0)
+        drain_dz(0, 1, 0, "S")
+        multiply_r(1, 0, 3)
+        add_r(1, 0, 3)
+        load_delta(1)
+        multiply_r(1, 0, 1)
+        add_r(1, 0, 1)
+        quant_dzt(0, 1)
+        multiply_r(1, 1, 2)
+        weave_u(1, 0, 0, 512, "S")
+        turn_b(0, 1)
+        drain_b(0, 1, "S")
+        times_delta(1, 0, "half", 0)
+        turn_b(1, 1)
+        drain_b(1, 1, "S")
+        multiply_du(0, 2, 1)
+        drain_du(0, 2, 1, "S")
+        multiply_r(1, 1, 1)
+        weave_dz(1, 0, 0, 256, "S")
+        multiply_du(0, 3, 1)
         multiply_du(0, 1, 1)
-        drain_du(0, 1, 1, 0, 128, "S")
-        quant_dzm(1, 0)
-        multiply_db(4, 0)
-        drain_db(4, 0, "S")
+        add_r(1, 1, 2)
+        drain_du(0, 3, 1, "S")
+        drain_du(0, 1, 1, "S")
+        quant_b(0)
+        multiply_du(0, 3, 0)
+        drain_du(0, 3, 0, "S")
+        store_du(0, 3)
+        multiply_du(0, 0, 1)
+        drain_du(0, 0, 1, "S")
         add_r(1, 1, 1)
+        multiply_du(0, 0, 0)
+        drain_du(0, 0, 0, "S")
+        store_du(0, 0)
+        multiply_du(0, 2, 0)
+        drain_du(0, 2, 0, "S")
+        store_du(0, 2)
+        times_delta(1, 0, "half", 1)
+        weave_dz(0, 1, 256, 512, "S")
+        multiply_r(1, 1, 3)
+        quant_u(1, 1)
+        weave_dz(1, 0, 256, 512, "V")
+        multiply_du(0, 1, 0)
+        weave_dz(0, 1, 0, 256, "V")
+        drain_du(0, 1, 0, "S")
+        quant_dzm(1, 0)
+        multiply_db(7, 0)
+        add_r(1, 1, 3)
+        drain_db(7, 0, "S")
         multiply_db(5, 0)
+        multiply_db(4, 0)
         drain_db(5, 0, "S")
+        drain_db(4, 0, "S")
         store_du(0, 1)
         store_db(2, 0)
-        multiply_db(6, 0)
-        drain_db(6, 0, "S")
-        multiply_db(7, 0)
-        drain_db(7, 0, "S")
-        store_db(3, 0)
-        times_delta(1, 1, "slot", 2)
         quant_u(1, 0)
-        multiply_db(1, 0)
-        drain_db(1, 0, "S")
-        multiply_db(0, 0)
-        drain_db(0, 0, "S")
-        store_db(0, 0)
-        drain_dz(1, 0, 1, "S")
-        times_delta(1, 1, "slot", 1)
-        multiply_db(2, 0)
-        drain_db(2, 0, "S")
         multiply_db(3, 0)
         drain_db(3, 0, "S")
+        multiply_db(6, 0)
+        multiply_db(2, 0)
+        drain_db(6, 0, "S")
+        store_db(3, 0)
+        drain_db(2, 0, "S")
         store_db(1, 0)
-        times_delta(1, 1, "slot", 0)
-        turn_dz(1, 1, 0)
+        multiply_db(1, 0)
+        multiply_db(0, 0)
+        drain_db(1, 0, "S")
+        drain_db(0, 0, "S")
+        store_db(0, 0)
         times_delta(1, 1, "slot", 3)
+        turn_dz(1, 0, 1)
+        times_delta(1, 1, "slot", 0)
+        times_delta(1, 1, "slot", 1)
+        turn_dz(1, 1, 0)
+        turn_dz(1, 0, 0)
+        times_delta(1, 1, "slot", 2)
+        turn_dz(1, 1, 1)
+        quant_dzm(0, 1)
         weave_dz(1, 1, 0, 256, "V")
         weave_dz(1, 1, 256, 512, "V")
-        turn_dz(1, 1, 1)
-        turn_dz(1, 0, 0)
         quant_dzm(1, 1)
-        multiply_db(4, 1)
-        drain_dz(1, 1, 0, "V")
-        drain_db(4, 1, "V")
-        drain_dz(1, 0, 0, "S")
-        multiply_db(5, 1)
-        drain_db(5, 1, "S")
-        store_db(2, 1)
+        multiply_db(7, 1)
+        drain_dz(1, 0, 1, "V")
+        drain_db(7, 1, "V")
+        drain_dz(1, 0, 0, "V")
+        drain_dz(1, 1, 1, "S")
+        drain_dz(1, 1, 0, "S")
+        multiply_db(6, 1)
+        drain_db(6, 1, "S")
+        store_db(3, 1)
+        multiply_db(3, 1)
+        drain_db(3, 1, "S")
+        multiply_db(2, 1)
+        drain_db(2, 1, "S")
+        store_db(1, 1)
         multiply_db(1, 1)
         drain_db(1, 1, "S")
         multiply_db(0, 1)
         drain_db(0, 1, "S")
         store_db(0, 1)
-        multiply_db(2, 1)
-        drain_db(2, 1, "S")
-        multiply_db(3, 1)
-        drain_db(3, 1, "S")
-        store_db(1, 1)
-        quant_dzt(1, 0)
-        drain_dz(1, 1, 1, "V")
         quant_dzt(1, 1)
-        multiply_du(1, 2, 0)
-        drain_du(1, 2, 0, 0, 128, "V")
-        multiply_du(1, 2, 1)
-        drain_du(1, 2, 1, 0, 128, "S")
-        multiply_db(7, 1)
-        drain_db(7, 1, "V")
-        multiply_db(6, 1)
-        store_du(1, 2)
+        quant_dzt(1, 0)
         multiply_du(1, 1, 0)
-        drain_db(6, 1, "V")
-        store_db(3, 1)
-        drain_du(1, 1, 0, 0, 128, "V")
+        drain_du(1, 1, 0, "S")
         multiply_du(1, 1, 1)
-        drain_du(1, 1, 1, 0, 128, "S")
+        drain_du(1, 1, 1, "V")
         store_du(1, 1)
-        multiply_du(1, 0, 0)
-        drain_du(1, 0, 0, 0, 128, "V")
-        multiply_du(1, 3, 1)
-        drain_du(1, 3, 1, 0, 128, "S")
-        store_du_half(1, 3, 1)
-        multiply_du(1, 3, 0)
-        drain_du(1, 3, 0, 0, 128, "V")
-        store_du_half(1, 3, 0)
+        multiply_db(4, 1)
+        drain_db(4, 1, "S")
+        multiply_db(5, 1)
         multiply_du(1, 0, 1)
-        drain_du(1, 0, 1, 0, 128, "S")
+        drain_du(1, 0, 1, "S")
+        drain_db(5, 1, "V")
+        store_db(2, 1)
+        multiply_du(1, 0, 0)
+        drain_du(1, 0, 0, "S")
         store_du(1, 0)
+        multiply_du(1, 2, 1)
+        multiply_du(1, 3, 0)
+        drain_du(1, 3, 0, "V")
+        store_du_half(1, 3, 0)
+        drain_du(1, 2, 1, "V")
+        multiply_du(1, 3, 1)
+        drain_du(1, 3, 1, "S")
+        store_du_half(1, 3, 1)
+        multiply_du(1, 2, 0)
+        drain_du(1, 2, 0, "S")
+        store_du(1, 2)

from contextlib import ExitStack

import concourse.mybir as mybir
from concourse.masks import make_identity

M, P_CH, N, D = 1024, 2048, 1024, 1024
FLOPS = 2 * M * N * P_CH + 2 * M * N * D + 2 * M * N * D

F32 = mybir.dt.float32
BF16 = mybir.dt.bfloat16
U32 = mybir.dt.uint32
U8 = mybir.dt.uint8
E4 = mybir.dt.float8_e4m3fn_x4
E5 = mybir.dt.float8_e5m2_x4
MULT = mybir.AluOpType.mult
ADD = mybir.AluOpType.add


def tile_state_space_backward_s6_kernel(tc, dy, c, ds_next, decay, delta, b, u, du, db):
    nc = tc.nc
    with ExitStack() as ctx:
        keep = ctx.enter_context(tc.tile_pool(name="keep", bufs=1))
        raw = ctx.enter_context(tc.tile_pool(name="raw", bufs=12))
        stage = ctx.enter_context(tc.tile_pool(name="stage", bufs=3))
        pairs = ctx.enter_context(tc.tile_pool(name="pairs", bufs=2))
        wove = ctx.enter_context(tc.tile_pool(name="wove", bufs=3))
        dzp = ctx.enter_context(tc.tile_pool(name="dzp", bufs=2))
        codes512 = ctx.enter_context(tc.tile_pool(name="codes512", bufs=10))
        psum = ctx.enter_context(tc.psum_pool(name="psum", bufs=4))
        ctx.enter_context(tc.manual_schedule())

        c_v = c.rearrange("(h p a) k -> h p a k", h=2, a=4)
        dy_v = dy.rearrange("(g p t) k -> g p t k", g=2, t=4)
        ds_v = ds_next.rearrange("(g p t) n -> g p t n", g=2, t=4)
        delta_v = delta.rearrange("(g p t) n -> g p t n", g=2, t=4)
        b_v = b.rearrange("(w x p y) n -> w p x y n", w=2, x=2, y=2)
        u_v = u.rearrange("(g p j) d -> g p j d", g=2, j=4)
        du_v = du.rearrange("(g p t) d -> g p t d", g=2, t=4)
        db_v = db.rearrange("(a p) n -> p a n", p=128)

        dec_rows = keep.tile([128, 128], BF16, name="dec_rows")
        nc.vector.memset(dec_rows[:], 0.0)
        ident = keep.tile([128, 128], F32, name="ident")
        make_identity(nc, ident[:])
        ident_h = keep.tile([128, 128], BF16, name="ident_h")
        nc.vector.tensor_copy(out=ident_h[:], in_=ident[:])
        dec_bc = keep.tile([128, 1024], BF16, name="dec_bc")
        dcol = keep.tile([128, 8], BF16, name="dcol")

        def codes(name, width, e):
            w = keep.tile([128, width], U32, name=name + "_codes", align_bytes=64)
            s = keep.tile([128, width], U8, name=name + "_scales", align_bytes=64)
            return w, s, e

        c_q = [codes("c%d" % h, 4 * 512, E4) for h in range(2)]
        b_q = [codes("b%d" % w, 2 * 512, E4) for w in range(2)]
        u_q = [codes("u%d" % g, 1024, E4) for g in range(2)]
        dy_q, dzm_q, dzt_q = {}, {}, {}

        def quant(dst, at, n, src):
            w, s, e = dst
            nc.vector.quantize_mx(out=w[:, at : at + n].bitcast(e), scales=s[:, at : at + n], in_=src)

        def quant_e5m2(store, key, src):
            w = codes512.tile([128, 512], U32, name="w512", align_bytes=64)
            s = codes512.tile([128, 512], U8, name="s512", align_bytes=64)
            store[key] = w, s, E5
            quant(store[key], 0, 512, src)

        def mx(out, lhs, lat, rhs, rat, first, last):
            lw, ls, le = lhs
            rw, rs, re = rhs
            nc.tensor.matmul_mx(
                out=out,
                lhsT=lw[:, lat : lat + 128].bitcast(le),
                lhsT_scale=ls[:, lat : lat + 128],
                rhs=rw[:, rat : rat + 512].bitcast(re),
                rhs_scale=rs[:, rat : rat + 512],
                start=first,
                stop=last,
            )

        def copy(eng, out, in_):
            if eng == "S":
                nc.scalar.copy(out=out, in_=in_)
            else:
                nc.vector.tensor_copy(out=out, in_=in_)

        c_raw, dy_raw, ds_raw, delta_raw, b_raw, u_raw = {}, {}, {}, {}, {}, {}
        banks, staged, accs, t1, dz, woven, out_rows = {}, {}, {}, {}, {}, {}, {}

        def load(store, key, view, parts):
            if key not in store:
                store[key] = raw.tile([128, 4, 1024], BF16, name="raw", align_bytes=64)
            rows = view.shape[1]
            flat = store[key][:].rearrange("p a n -> p (a n)").rearrange("p (a n) -> p a n", a=rows)
            for a0, a1, k0, k1 in parts:
                nc.sync.dma_start(out=flat[:, a0:a1, k0:k1], in_=view[:, a0:a1, k0:k1])

        def load_c(h, q, *parts):
            load(c_raw, (h, q), c_v[h][:, 2 * q : 2 * q + 2, :], parts)

        def load_dy(g, q, *parts):
            load(dy_raw, (g, q), dy_v[g][:, 2 * q : 2 * q + 2, :], parts)

        def load_ds(g):
            load(ds_raw, g, ds_v[g], [(0, 4, 0, 1024)])

        def load_delta(g):
            load(delta_raw, g, delta_v[g], [(0, 4, 0, 1024)])

        def load_b(w):
            b_raw[w] = raw.tile([128, 4, 1024], BF16, name="raw", align_bytes=64)
            nc.sync.dma_start(out=b_raw[w][:].rearrange("p (x y) n -> p x y n", x=2), in_=b_v[w])

        def load_u(g):
            load(u_raw, g, u_v[g], [(0, 4, 0, 1024)])

        def load_decay():
            nc.sync.dma_start(out=dec_rows[0:8, :], in_=decay.rearrange("(a p) -> a p", p=128))

        def words_of(t):
            return t[:].rearrange("p a n -> p (a n)").bitcast(F32)

        def turn(key, words, base, step):
            bank = psum.tile([128, 2, 2, 128], F32, name="tp")
            for x in range(2):
                for v in range(2):
                    lo = base + 256 * x + (v if step == 2 else 128 * v)
                    hi = base + 256 * x + 256 if step == 2 else lo + 128
                    nc.tensor.transpose(bank[:, x, v, :], words[:, lo:hi:step], ident[:])
            banks[key] = bank

        def turn_c(h, a, half):
            turn(("c", h, a, half), words_of(c_raw[h, a // 2]), 1024 * (a % 2) + 512 * half, 2)

        def turn_dy(g, s, half):
            turn(("dy", g, s, half), words_of(dy_raw[g, s // 2]), 1024 * (s % 2) + 512 * half, 2)

        def turn_b(i, half):
            turn(("b", i, half), words_of(b_raw[i // 2]), 512 * (2 * (i % 2) + half), 2)

        def turn_dz(g, h, half):
            turn(("dz", g, h, half), words_of(dz[g, h]), 512 * half, 1)

        def drain_c(h, a, half, eng):
            if ("c", h, a // 2) not in staged:
                staged["c", h, a // 2] = pairs.tile([128, 4096], BF16, name="xc", align_bytes=64)
            xw = staged["c", h, a // 2][:].bitcast(F32).rearrange("p (k r v) -> p k r v", k=4, v=2)
            copy(
                eng,
                xw[:, 2 * half : 2 * half + 2, 128 * (a % 2) : 128 * (a % 2) + 128, :],
                banks["c", h, a, half][:].rearrange("p k v r -> p k r v"),
            )

        def drain_rows(key, half, eng):
            if key not in staged:
                staged[key] = stage.tile([128, 2048], BF16, name="xt", align_bytes=64)
            xw = staged[key][:].bitcast(F32).rearrange("p (k r v) -> p k r v", k=4, v=2)
            copy(eng, xw[:, 2 * half : 2 * half + 2], banks[key + (half,)][:].rearrange("p k v r -> p k r v"))

        def drain_dy(g, s, half, eng):
            drain_rows(("dy", g, s), half, eng)

        def drain_dz(g, h, half, eng):
            drain_rows(("dz", g, h), half, eng)

        def drain_b(i, half, eng):
            w, r0 = i // 2, 256 * (i % 2) + 128 * half
            if ("b", w) not in staged:
                staged["b", w] = pairs.tile([128, 4096], BF16, name="xc", align_bytes=64)
            xw = staged["b", w][:].bitcast(F32).rearrange("p (k r v) -> p k r v", k=2, v=2)
            copy(
                eng,
                xw[:, :, r0 : r0 + 128, :],
                banks["b", i, half][:].rearrange("p k v r -> p k r v"),
            )

        def quant_c(h, j):
            for k in range(4):
                quant(c_q[h], 512 * k + 256 * j, 256, staged["c", h, j][:, 1024 * k : 1024 * k + 1024])

        def quant_dy(g, s):
            quant_e5m2(dy_q, (g, s), staged["dy", g, s][:])

        def quant_b(w):
            quant(b_q[w], 0, 1024, staged["b", w][:])

        def quant_dzt(g, h):
            quant_e5m2(dzt_q, (g, h), staged["dz", g, h][:])

        def decay_turn():
            accs["dcol"] = psum.tile([128, 128], BF16, name="acc")
            nc.tensor.transpose(accs["dcol"][:], dec_rows[:], ident_h[:])

        def decay_col():
            nc.vector.tensor_copy(out=dcol[:], in_=accs["dcol"][:, 0:8])

        def decay_spread():
            accs["dec"] = psum.tile([128, 8, 128], BF16, name="acc")
            for a in range(8):
                nc.tensor.transpose(accs["dec"][:, a, :], dcol[:, a : a + 1].to_broadcast([128, 128]), ident_h[:])

        def decay_rows():
            nc.vector.tensor_copy(out=dec_bc[:], in_=accs["dec"][:].rearrange("p a r -> p (a r)"))

        def decay_part(g, h, v):
            if (g, h) not in t1:
                t1[g, h] = dzp.tile([128, 4, 512], F32, name="t1")
            nc.vector.tensor_tensor(
                out=t1[g, h][:, :, 256 * v : 256 * v + 256].rearrange("m s (p e) -> m s p e", e=2),
                in0=ds_raw[g][:, :, 512 * h : 512 * h + 512].rearrange("m s (p v e) -> m s v p e", v=2, e=2)[:, :, v],
                in1=dec_bc[:, 512 * h : 512 * h + 512]
                .rearrange("m (p v e) -> m v p e", v=2, e=2)[:, v]
                .unsqueeze(1)
                .to_broadcast([128, 4, 128, 2]),
                op=MULT,
            )

        def multiply_r(g, h, s):
            accs["r", g, h, s] = psum.tile([128, 512], F32, name="acc")
            for k in range(4):
                mx(accs["r", g, h, s][:], dy_q[g, s], 128 * k, c_q[h], 512 * k, k == 0, k == 3)

        def add_r(g, h, s):
            row = t1[g, h][:, s, :].rearrange("m (v p e) -> m v p e", v=2, e=2)
            nc.vector.tensor_tensor(
                out=row,
                in0=accs["r", g, h, s][:].rearrange("m (v e p) -> m v p e", v=2, e=2),
                in1=row,
                op=ADD,
            )

        def times_delta(g, h, kind, i):
            if (g, h) not in dz:
                dz[g, h] = dzp.tile([128, 4, 512], BF16, name="dz", align_bytes=64)
            to, ds = dz[g, h][:], t1[g, h][:]
            delta_h = delta_raw[g][:, :, 512 * h : 512 * h + 512].rearrange("m s (p v e) -> m s v p e", v=2, e=2)
            if kind == "slot":
                to, ds = (x[:, i, :].rearrange("m (v p e) -> m v p e", v=2, e=2) for x in (to, ds))
                factor = delta_h[:, i]
            else:
                half = slice(256 * i, 256 * i + 256)
                to, ds = (x[:, :, half].rearrange("m s (p e) -> m s p e", e=2) for x in (to, ds))
                factor = delta_h[:, :, i]
            nc.vector.tensor_tensor(out=to, in0=ds, in1=factor, op=MULT)

        def weave(key, src, n0, n1, eng):
            if key not in woven:
                woven[key] = wove.tile([128, 2048], BF16, name="wv", align_bytes=64)
            copy(
                eng,
                woven[key][:, 4 * n0 : 4 * n1].rearrange("p (n t) -> p n t", t=4),
                src[:, :, n0:n1].rearrange("p t n -> p n t"),
            )

        def weave_dz(g, h, n0, n1, eng):
            weave(("dz", g, h), dz[g, h][:], n0, n1, eng)

        def weave_u(g, w, n0, n1, eng):
            weave(("u", g, w), u_raw[g][:, :, 512 * w : 512 * w + 512], n0, n1, eng)

        def quant_dzm(g, h):
            quant_e5m2(dzm_q, (g, h), woven["dz", g, h][:])

        def quant_u(g, w):
            quant(u_q[g], 512 * w, 512, woven["u", g, w][:])

        def multiply_du(g, s, w):
            accs["du", g, s, w] = psum.tile([128, 512], F32, name="acc")
            for h in range(2):
                mx(accs["du", g, s, w][:], dzt_q[g, h], 128 * s, b_q[w], 512 * h, h == 0, h == 1)

        def out_tile(key):
            if key not in out_rows:
                out_rows[key] = raw.tile([128, 2, 512], F32, name="raw", align_bytes=64)
            return out_rows[key]

        def drain_du(g, s, w, eng):
            row = out_tile(("du", g, s))
            copy(
                eng,
                row[:, w, :].rearrange("m (x p y) -> m x p y", x=2, y=2),
                accs["du", g, s, w][:].rearrange("m (x y p) -> m x p y", x=2, y=2),
            )

        def store_du(g, s):
            nc.sync.dma_start(out=du_v[g][:, s, :], in_=out_rows["du", g, s][:].rearrange("m w d -> m (w d)"))

        def store_du_half(g, s, w):
            nc.sync.dma_start(out=du_v[g][:, s, 512 * w : 512 * w + 512], in_=out_rows["du", g, s][:, w, :])

        def multiply_db(a, h):
            accs["db", a, h] = psum.tile([128, 512], F32, name="acc")
            for g in range(2):
                mx(accs["db", a, h][:], u_q[g], 128 * a, dzm_q[g, h], 0, g == 0, g == 1)

        def drain_db(a, h, eng):
            rows = out_tile(("db", h, a // 2))
            copy(
                eng,
                rows[:, a % 2, :].rearrange("m (p v e) -> m p v e", v=2, e=2),
                accs["db", a, h][:].rearrange("m (v p e) -> m p v e", v=2, e=2),
            )

        def store_db(j, h):
            nc.sync.dma_start(out=db_v[:, 2 * j : 2 * j + 2, 512 * h : 512 * h + 512], in_=out_rows["db", h, j][:])

        load_dy(0, 0, (1, 2, 0, 2048))
        turn_dy(0, 1, 1)
        turn_dy(0, 1, 0)
        drain_dy(0, 1, 0, "S")
        load_c(0, 0, (0, 1, 0, 2048))
        drain_dy(0, 1, 1, "V")
        turn_c(0, 0, 0)
        turn_c(0, 0, 1)
        drain_c(0, 0, 1, "S")
        drain_c(0, 0, 0, "V")
        load_dy(0, 1, (1, 2, 0, 2048))
        turn_dy(0, 3, 1)
        drain_dy(0, 3, 1, "S")
        turn_dy(0, 3, 0)
        drain_dy(0, 3, 0, "S")
        quant_dy(0, 3)
        load_c(0, 1, (1, 2, 0, 2048))
        turn_c(0, 3, 0)
        load_dy(0, 1, (0, 1, 0, 2048))
        quant_dy(0, 1)
        drain_c(0, 3, 0, "V")
        turn_dy(0, 2, 1)
        drain_dy(0, 2, 1, "V")
        load_decay()
        decay_turn()
        turn_c(0, 3, 1)
        drain_c(0, 3, 1, "S")
        decay_col()
        turn_dy(0, 2, 0)
        drain_dy(0, 2, 0, "S")
        load_c(0, 0, (1, 2, 0, 2048))
        turn_c(0, 1, 0)
        quant_dy(0, 2)
        drain_c(0, 1, 0, "S")
        turn_c(0, 1, 1)
        drain_c(0, 1, 1, "S")
        quant_c(0, 0)
        load_c(0, 1, (0, 1, 1024, 2048))
        load_c(0, 1, (0, 1, 0, 1024))
        turn_c(0, 2, 1)
        turn_c(0, 2, 0)
        drain_c(0, 2, 0, "S")
        drain_c(0, 2, 1, "S")
        load_c(1, 1, (1, 2, 0, 2048))
        turn_c(1, 3, 0)
        quant_c(0, 1)
        turn_c(1, 3, 1)
        drain_c(1, 3, 1, "S")
        decay_spread()
        load_dy(0, 0, (0, 1, 0, 2048))
        turn_dy(0, 0, 0)
        decay_rows()
        drain_dy(0, 0, 0, "S")
        drain_c(1, 3, 0, "S")
        multiply_r(0, 0, 3)
        turn_dy(0, 0, 1)
        load_ds(0)
        decay_part(0, 0, 0)
        load_c(1, 0, (1, 2, 0, 2048))
        turn_c(1, 1, 0)
        drain_c(1, 1, 0, "S")
        turn_c(1, 1, 1)
        drain_dy(0, 0, 1, "S")
        decay_part(0, 1, 1)
        drain_c(1, 1, 1, "S")
        multiply_r(0, 0, 1)
        load_c(1, 1, (0, 1, 0, 2048))
        turn_c(1, 2, 0)
        drain_c(1, 2, 0, "S")
        turn_c(1, 2, 1)
        drain_c(1, 2, 1, "S")
        decay_part(0, 0, 1)
        decay_part(0, 1, 0)
        load_c(1, 0, (0, 1, 0, 2048))
        turn_c(1, 0, 1)
        drain_c(1, 0, 1, "S")
        quant_dy(0, 0)
        turn_c(1, 0, 0)
        add_r(0, 0, 3)
        add_r(0, 0, 1)
        quant_c(1, 1)
        drain_c(1, 0, 0, "S")
        quant_c(1, 0)
        multiply_r(0, 0, 2)
        multiply_r(0, 0, 0)
        add_r(0, 0, 0)
        add_r(0, 0, 2)
        load_u(0)
        weave_u(0, 1, 0, 512, "S")
        quant_u(0, 1)
        load_dy(1, 0, (0, 2, 0, 2048))
        turn_dy(1, 0, 1)
        turn_dy(1, 0, 0)
        drain_dy(1, 0, 0, "S")
        turn_dy(1, 1, 1)
        multiply_r(0, 1, 0)
        multiply_r(0, 1, 2)
        multiply_r(0, 1, 1)
        load_delta(0)
        times_delta(0, 0, "half", 0)
        add_r(0, 1, 0)
        times_delta(0, 0, "half", 1)
        weave_u(0, 0, 0, 512, "S")
        quant_u(0, 0)
        turn_dy(1, 1, 0)
        turn_dz(0, 0, 1)
        add_r(0, 1, 1)
        drain_dy(1, 0, 1, "S")
        quant_dy(1, 0)
        load_dy(1, 1, (0, 2, 0, 2048))
        turn_dy(1, 2, 1)
        weave_dz(0, 0, 0, 256, "S")
        multiply_r(0, 1, 3)
        drain_dy(1, 1, 1, "S")
        drain_dy(1, 1, 0, "S")
        add_r(0, 1, 2)
        load_ds(1)
        decay_part(1, 0, 1)
        add_r(0, 1, 3)
        quant_dy(1, 1)
        times_delta(0, 1, "half", 0)
        decay_part(1, 0, 0)
        drain_dz(0, 0, 1, "S")
        drain_dy(1, 2, 1, "S")
        weave_dz(0, 0, 256, 512, "S")
        turn_dy(1, 3, 1)
        turn_dz(0, 0, 0)
        drain_dy(1, 3, 1, "S")
        drain_dz(0, 0, 0, "S")
        multiply_r(1, 1, 0)
        times_delta(0, 1, "half", 1)
        quant_dzt(0, 0)
        turn_dy(1, 2, 0)
        drain_dy(1, 2, 0, "S")
        quant_dy(1, 2)
        load_b(0)
        turn_b(1, 0)
        drain_b(1, 0, "S")
        load_b(1)
        turn_b(2, 0)
        drain_b(2, 0, "S")
        turn_dy(1, 3, 0)
        decay_part(1, 1, 1)
        drain_dy(1, 3, 0, "S")
        load_u(1)
        weave_u(1, 1, 0, 512, "S")
        multiply_r(1, 0, 0)
        add_r(1, 0, 0)
        turn_b(0, 0)
        drain_b(0, 0, "S")
        quant_dy(1, 3)
        turn_dz(0, 1, 1)
        drain_dz(0, 1, 1, "S")
        decay_part(1, 1, 0)
        quant_dzm(0, 0)
        add_r(1, 1, 0)
        turn_b(3, 1)
        multiply_r(1, 0, 2)
        turn_b(3, 0)
        add_r(1, 0, 2)
        turn_b(2, 1)
        drain_b(3, 1, "S")
        drain_b(3, 0, "S")
        drain_b(2, 1, "S")
        quant_b(1)
        turn_dz(0, 1, 0)
        drain_dz(0, 1, 0, "S")
        multiply_r(1, 0, 3)
        add_r(1, 0, 3)
        load_delta(1)
        multiply_r(1, 0, 1)
        add_r(1, 0, 1)
        quant_dzt(0, 1)
        multiply_r(1, 1, 2)
        weave_u(1, 0, 0, 512, "S")
        turn_b(0, 1)
        drain_b(0, 1, "S")
        times_delta(1, 0, "half", 0)
        turn_b(1, 1)
        drain_b(1, 1, "S")
        multiply_du(0, 2, 1)
        drain_du(0, 2, 1, "S")
        multiply_r(1, 1, 1)
        weave_dz(1, 0, 0, 256, "S")
        multiply_du(0, 3, 1)
        multiply_du(0, 1, 1)
        add_r(1, 1, 2)
        drain_du(0, 3, 1, "S")
        drain_du(0, 1, 1, "S")
        quant_b(0)
        multiply_du(0, 3, 0)
        drain_du(0, 3, 0, "S")
        store_du(0, 3)
        multiply_du(0, 0, 1)
        drain_du(0, 0, 1, "S")
        add_r(1, 1, 1)
        multiply_du(0, 0, 0)
        drain_du(0, 0, 0, "S")
        store_du(0, 0)
        multiply_du(0, 2, 0)
        drain_du(0, 2, 0, "S")
        store_du(0, 2)
        times_delta(1, 0, "half", 1)
        weave_dz(0, 1, 256, 512, "S")
        multiply_r(1, 1, 3)
        quant_u(1, 1)
        weave_dz(1, 0, 256, 512, "V")
        multiply_du(0, 1, 0)
        weave_dz(0, 1, 0, 256, "V")
        drain_du(0, 1, 0, "S")
        quant_dzm(1, 0)
        multiply_db(7, 0)
        add_r(1, 1, 3)
        drain_db(7, 0, "S")
        multiply_db(5, 0)
        multiply_db(4, 0)
        drain_db(5, 0, "S")
        drain_db(4, 0, "S")
        store_du(0, 1)
        store_db(2, 0)
        quant_u(1, 0)
        multiply_db(3, 0)
        drain_db(3, 0, "S")
        multiply_db(6, 0)
        multiply_db(2, 0)
        drain_db(6, 0, "S")
        store_db(3, 0)
        drain_db(2, 0, "S")
        store_db(1, 0)
        multiply_db(1, 0)
        multiply_db(0, 0)
        drain_db(1, 0, "S")
        drain_db(0, 0, "S")
        store_db(0, 0)
        times_delta(1, 1, "slot", 3)
        turn_dz(1, 0, 1)
        times_delta(1, 1, "slot", 0)
        times_delta(1, 1, "slot", 1)
        turn_dz(1, 1, 0)
        turn_dz(1, 0, 0)
        times_delta(1, 1, "slot", 2)
        turn_dz(1, 1, 1)
        quant_dzm(0, 1)
        weave_dz(1, 1, 0, 256, "V")
        weave_dz(1, 1, 256, 512, "V")
        quant_dzm(1, 1)
        multiply_db(7, 1)
        drain_dz(1, 0, 1, "V")
        drain_db(7, 1, "V")
        drain_dz(1, 0, 0, "V")
        drain_dz(1, 1, 1, "S")
        drain_dz(1, 1, 0, "S")
        multiply_db(6, 1)
        drain_db(6, 1, "S")
        store_db(3, 1)
        multiply_db(3, 1)
        drain_db(3, 1, "S")
        multiply_db(2, 1)
        drain_db(2, 1, "S")
        store_db(1, 1)
        multiply_db(1, 1)
        drain_db(1, 1, "S")
        multiply_db(0, 1)
        drain_db(0, 1, "S")
        store_db(0, 1)
        quant_dzt(1, 1)
        quant_dzt(1, 0)
        multiply_du(1, 1, 0)
        drain_du(1, 1, 0, "S")
        multiply_du(1, 1, 1)
        drain_du(1, 1, 1, "V")
        store_du(1, 1)
        multiply_db(4, 1)
        drain_db(4, 1, "S")
        multiply_db(5, 1)
        multiply_du(1, 0, 1)
        drain_du(1, 0, 1, "S")
        drain_db(5, 1, "V")
        store_db(2, 1)
        multiply_du(1, 0, 0)
        drain_du(1, 0, 0, "S")
        store_du(1, 0)
        multiply_du(1, 2, 1)
        multiply_du(1, 3, 0)
        drain_du(1, 3, 0, "V")
        store_du_half(1, 3, 0)
        drain_du(1, 2, 1, "V")
        multiply_du(1, 3, 1)
        drain_du(1, 3, 1, "S")
        store_du_half(1, 3, 1)
        multiply_du(1, 2, 0)
        drain_du(1, 2, 0, "S")
        store_du(1, 2)
